import numpy as np, ml_dtypes
CORES = [83,85,87,115,117,119]
N = 6
BF = ml_dtypes.bfloat16
S, A, L, M, R, D = 128, 64, 32, 4, 64, 32
def steps(nx, sy):
    g = np.arange(8); s = np.zeros(8, np.int64); place = np.zeros((N * L, 8), np.int64); cnt = np.zeros((N * L, 8), np.int64)
    for i in range(N * L):
        place[i] = sy[i // L, :, i % L].astype(np.int64) * S + s
        v = nx[i // L, g, place[i]].astype(np.int64)
        s = v % S; cnt[i] = v // S
    return place, cnt
def counts(rng, uneven=False):
    k = np.argsort(rng.random((N, 8, S, A)), -1)
    w = rng.integers(0, 2, k.shape) * M if uneven else rng.integers(0, M + 1, k.shape)
    return np.ascontiguousarray(np.where(k <= M, k, w).transpose(0, 1, 3, 2))
def perms(rng):
    return np.argsort(rng.random((N, 8, A, S)), -1)
def bounds(rng):
    e = np.zeros((8, N + 1), np.int64)
    e[:, 1:N] = np.arange(1, N) * R + rng.integers(-D, D + 1, (8, N - 1)); e[:, N] = N * R - rng.integers(0, D + 1, 8)
    e[0, N] = N * R - D; e[7, N] = N * R
    return e
def draw(rng, to, ct, e, burst=False):
    n = (e[:, 1:] - e[:, :-1])[:, :, None]
    k = (np.arange(L * M) - M * rng.integers(0, L, (8, N, 1))) % (L * M) if burst else np.argsort(rng.random((8, N, L * M)), -1)
    c = np.sum((k < n).reshape(8, N, L, M), axis=-1)
    g = np.arange(8); s = np.zeros(8, np.int64); sy = np.zeros((N, 8, L), np.int32)
    for i in range(N * L):
        q = i // L; ok = ct[q][g, :, s] == c[:, q, i % L][:, None]
        a = np.argmax(np.where(ok, rng.random((8, A)), -1.0), axis=1)
        sy[q, :, i % L] = a; s = to[q][g, a, s]
    return {"nx": (ct * S + to).reshape(N, 8, A * S).astype(np.int32), "em": rng.integers(0, 64 ** M, (N, 8, A * S)).astype(np.int32), "sy": sy}
def setup_inputs(rng):
    to = np.where(rng.random((N, 8, A, 1)) < 0.125, rng.integers(0, S, (N, 8, A, S)), perms(rng))
    return draw(rng, to, counts(rng), bounds(rng))
def setup_inputs_edge(rng):
    e = bounds(rng); g = np.arange(8)[:, None]; r = np.arange(1, N)[None, :]
    e[:, 1:N] = r * R + D * np.where(g % 2 == 0, 1 - 2 * ((r + g // 2) % 2), 1 - 2 * (g // 2 % 2)); e[:, N] = N * R - D * (np.arange(8) // 4)
    return draw(rng, perms(rng), counts(rng), e)
def setup_inputs_even(rng):
    e = bounds(rng); e[:] = np.arange(N + 1) * R
    return draw(rng, perms(rng), counts(rng), e)
def setup_inputs_merge(rng):
    kind = (np.argsort(rng.random((N, 8, A)), -1) % 4)[:, :, :, None]; h = (N, 8, A, 1); s = np.arange(S)
    one = np.where(rng.random(h) < 0.5, rng.integers(0, 2, h) * (S - 1), rng.integers(0, S, h))
    to = np.where(kind == 0, one, np.where(kind == 1, s, np.where(kind == 2, (s + 1) % S, rng.integers(0, S, (N, 8, A, S)))))
    return draw(rng, to, counts(rng), bounds(rng))
def setup_inputs_spread(rng):
    to = np.minimum(np.floor(S * rng.random((N, 8, A, S)) ** 6), S - 1).astype(np.int64)
    d = draw(rng, to, counts(rng, True), bounds(rng), True)
    h = (N, 8, A * S); d["em"] = (d["em"] >> np.where(rng.random(h) < 0.5, rng.integers(0, 6 * M, h), 0)).astype(np.int32)
    return d
def check_inputs(d):
    bad = []
    for k, top in (("nx", (M + 1) * S), ("em", 64 ** M), ("sy", A)):
        if d[k].min() < 0 or d[k].max() >= top: bad.append("range of " + k)
    if bad: return bad
    place, cnt = steps(d["nx"], d["sy"])
    off = np.add.accumulate(cnt, 0)[L - 1::L] - R * np.arange(1, N + 1)[:, None]
    if (np.abs(off) > D).any(): bad.append("running totals")
    if (off[-1] > 0).any(): bad.append("whole total")
    return bad
def reference(nx, em, sy):
    place, cnt = steps(nx, sy); g = np.broadcast_to(np.arange(8), (N * L, 8)); r = (np.arange(N * L) // L)[:, None]
    e = em[r, g, place].astype(np.int64); beg = np.add.accumulate(cnt, 0) - cnt
    z = np.full((8, N * R), -1, np.int64)
    for m in range(M):
        on = cnt > m
        z[g[on], beg[on] + m] = ((e >> (6 * m)) & 63)[on]
    return {"y": np.ascontiguousarray(z.reshape(8, N, R).transpose(1, 0, 2)).astype(np.float32)}

@@ -1,0 +1,371 @@
+from concourse.mybir import dt, AluOpType, AxisListType, ActivationFunctionType
+from concourse.bass import IndirectOffsetOnAxis, DstId, RemoteDMATransfer
+
+SCRATCH = {"emd": ("dram", [512, 128], "int32")}
+for _t, _l in (
+    ("int32", "TN:32,16 TS:32,16 SY:8,16 XI:16 XJ:16 HI:256 HJ:256 IDX:2 IDY:2 AE:256 EM:32 E2:2 D:8 P:1 PI:8 DIAG:16"),
+    ("bfloat16", "TB:32,16 CB:32,16 TBLK:32,32 SYM:8,32 OA:128 O:128 OM:256 XS:32 XR:256 XQ1:128 XQ2:128 CF:160 TO:256 "
+                 "CO:256 CA:16 CC:16 GTB:64 VB:64 OH0:132 OH1:132 ZB:8 ZP:8 ZN:8 ONES:256 L2A:128 L2:128 SELW:192 BLKA:128 "
+                 "BLK:128 IOTA2:256 SHM:128 D0:128 TRI:128 B64A:64 B64:64 IOTAX:132 BC:1"),
+    ("uint16", "OFF:256 U0:2 U:160 TM:16 SA:16 SB:18 PERM:8 REP:4"),
+    ("float32", "INJ:4096 WA:256 WB:256 WIN1:128 WIN2:128 SO:256 GT:8 YS:64 ONEF:16 PF:12 IO16:16 MASKQ:16 IO2G:8 IOR:4 "
+                "R16A:16 R16:16 MT:4"),
+):
+    for _b in _l.split():
+        _n, _d = _b.split(":")
+        SCRATCH[_n] = ("sbuf", [128] + [int(_x) for _x in _d.split(",")], _t)
+for _b in range(8):
+    SCRATCH["B%d" % _b] = ("psum", [128, 512], "float32")
+SEMAPHORES = ["ldsy", "ldn0", "ldn1", "ldn2", "ldn3", "ldem", "ldidx", "v", "t", "s", "gq", "ge",
+              "arr0", "arr1", "arr2", "arr3", "arr4", "arrz", "lsf", "lsz", "st"]
+OP = AluOpType
+FN = ActivationFunctionType
+MOST = 8
+
+
+def common_mask(topo, src, dsts, most):
+    ok = [e for e in topo.engines(src, dsts[0]) if all(e in topo.engines(src, d) for d in dsts)][:most]
+    return sum(1 << e for e in ok), len(ok)
+
+
+def parts(topo, T, r):
+    me, later = T.cores[r], T.cores[r + 1:]
+    two = ([d for d in later if topo.chip(d) != topo.chip(me)], [d for d in later if topo.chip(d) == topo.chip(me)])
+    return [p for p in two if p]
+
+
+def beside(T, r):
+    return [x for x in (r - 1, r + 1) if 0 <= x < len(T.cores)]
+
+
+def dst_id(topo, d):
+    rid, pid, _ = topo.addr(d)
+    return DstId(rid=rid, pnc=pid)
+
+
+def rank_program(g, core, T, topo):
+    rank = T.rank_of(core)
+    if rank is None:
+        return
+    v, t, s, y = g.vector, g.tensor, g.scalar, g.sync
+    S = T.sem
+    N = len(T.cores)
+    cnt = {"v": 0, "t": 0, "s": 0, "gq": 0}
+    seen = {}
+    queues = {"v": v, "t": t, "s": s, "y": y, "g": g}
+
+    def inc(key, ins):
+        ins.then_inc(S[key], 1)
+        cnt[key] += 1
+        return cnt[key]
+
+    def vi(ins):
+        return inc("v", ins)
+
+    def ti(ins):
+        return inc("t", ins)
+
+    def si(ins):
+        return inc("s", ins)
+
+    def gi(ins):
+        return inc("gq", ins)
+
+    def need(q, key, n):
+        if n and seen.get((q, key), 0) < n:
+            queues[q].wait_ge(S[key], n)
+            seen[(q, key)] = n
+
+    def arrived(q, r):
+        for p in parts(topo, T, r):
+            if core in p:
+                need(q, "arr%d" % r, common_mask(topo, T.cores[r], p, MOST)[1])
+
+    y.dma_start(T.SY[0:1, :, :], T.sy[0::2, :]).then_inc(S.ldsy, 16)
+    s.dma_start(T.SY[1:2, :, :], T.sy[1::2, :]).then_inc(S.ldsy, 16)
+    for i in range(4):
+        (y, s)[i % 2].dma_start(T.TN[:, 8 * i:8 * i + 8, :], T.nx[2 * i:2 * i + 2, :]).then_inc(S["ldn%d" % i], 16)
+    for h in range(2):
+        y.dma_start(T.IDX[:, h:h + 1], T.sy[:, 16 * h:16 * h + 16]).then_inc(S.ldidx, 16)
+    y.dma_start(T.emd[:], T.em[:]).then_inc(S.ldem, 16)
+
+    vi(v.memset(T.ONES[:], 1.0))
+    v_ones = vi(v.memset(T.ONEF[:], 1.0))
+    gi(g.iota(T.P[:], [[1, 1]], 0, 1))
+    gIO = gi(g.iota(T.IO16[:], [[1, 16]], 0, 0, allow_small_or_imprecise_dtypes=True))
+    need("g", "v", v_ones)
+    n1 = gi(g.affine_select(T.L2A[0:2, :], T.ONES[0:2, 0:128], [[1, 128]], OP.is_ge, 0.0, 0, -64))
+    need("g", "gq", n1)
+    gL2 = gi(g.affine_select(T.L2[0:2, :], T.L2A[0:2, :], [[-1, 128]], OP.is_ge, 0.0, 63, 64))
+    vi(v.memset(T.TBLK[:], 0.0))
+    vi(v.memset(T.U0[:], 0))
+    vi(v.memset(T.BC[:], 2.0 - 4.0 * rank))
+    nblk = 0 if rank == 0 else (2 if rank > 4 else 1)
+    if nblk and 32 * rank < 128 * nblk:
+        vi(v.memset(T.XR[:, 32 * rank:128 * nblk], 0.0))
+    need("v", "gq", gIO)
+    for k, a in enumerate((15, 63, 1, 14)):
+        vi(v.tensor_scalar(T.PI[:, k:k + 1], T.P[:], a, None, OP.bitwise_and))
+    vi(v.tensor_scalar(T.PI[:, 4:5], T.P[:], 4, None, OP.logical_shift_right))
+    vP = vi(v.tensor_scalar(T.PI[:, 5:6], T.P[:], 3, 1, OP.logical_shift_right, OP.bitwise_and))
+    need("v", "v", vP)
+    vi(v.tensor_copy(T.PF[:, 0:6], T.PI[:, 0:6]))
+    vPF = vi(v.tensor_copy(T.PF[:, 6:7], T.P[:]))
+    need("v", "v", vPF)
+    vMQ = vi(v.tensor_scalar(T.MASKQ[:], T.IO16[:], T.PF[:, 0:1], None, OP.is_equal))
+    need("v", "ldsy", 32)
+    vi(v.tensor_copy(T.SYM[0:2, :, 0:16], T.SY[0:2, :, :]))
+    vSY = vi(v.tensor_scalar(T.SYM[0:2, :, 16:32], T.SY[0:2, :, :], 64.0, None, OP.add))
+    need("t", "gq", gL2)
+    need("t", "v", vSY)
+    tSY = ti(t.matmul(T.B0[:, 0:256], T.L2[0:2, :], T.SYM[0:2, :, :], True, True))
+    tSO = ti(t.matmul(T.B3[:, 0:128], T.L2[0:2, :], T.SYM[0:2, :, 0:16], True, True))
+    need("s", "t", tSO)
+    need("s", "v", vPF)
+    s1 = si(s.activation(T.OA[:], T.B3[:, 0:128], FN.Abs, bias=T.PF[:, 1:2], scale=-1.0))
+    need("s", "s", s1)
+    si(s.activation(T.O[:], T.OA[:], FN.Relu, bias=1.0, scale=-1.0))
+    vTB, sBLK = {}, {}
+    for i in range(4):
+        r8 = slice(8 * i, 8 * i + 8)
+        need("v", "ldn%d" % i, 16)
+        vTS = vi(v.tensor_scalar(T.TS[:, r8, :], T.TN[:, r8, :], 127, None, OP.bitwise_and))
+        if i == 0:
+            need("v", "t", tSY)
+            vi(v.tensor_scalar(T.OM[:], T.B0[:, 0:256], T.PF[:, 6:7], None, OP.is_equal))
+        vi(v.tensor_scalar(T.CB[:, r8, :], T.TN[:, r8, :], 1.0 / 128, 128.50390625, OP.mult, OP.add))
+        need("v", "v", vTS)
+        vTB[i] = vi(v.tensor_scalar(T.TB[:, r8, :], T.TS[:, r8, :], 128.0, None, OP.mult))
+        need("s", "v", vTB[i])
+        for x in range(2):
+            p = slice(64 * x, 64 * x + 64)
+            sBLK[i] = si(s.activation(T.TBLK[p, r8, 16 * x:16 * x + 16], T.TB[p, r8, :], FN.Copy, scale=1.0 / 128))
+    tA = tOFF = 0
+    for kind, i in (("A", 0), ("A", 1), ("F", 0), ("A", 2), ("F", 1), ("A", 3), ("F", 2), ("F", 3)):
+        r8 = slice(8 * i, 8 * i + 8)
+        if kind == "A":
+            need("t", "v", vTB[i])
+            for h in range(2):
+                k = 2 * i + h
+                a = T.B2[32 * i:32 * i + 32, 128 * h:128 * h + 128]
+                t.matmul(a, T.OM[:, 32 * k:32 * k + 32], T.TB[:, r8, :], True, False)
+                m = t.matmul(a, T.OM[:, 32 * k:32 * k + 32], T.CB[:, r8, :], False, True)
+            if i == 3:
+                tA = ti(m)
+        else:
+            need("t", "s", sBLK[i])
+            for c in range(8):
+                m = t.matmul(T.B1[32 * i:32 * i + 32, c:256:8], T.TBLK[:, 8 * i + c, :], T.O[:, 32 * i:32 * i + 32],
+                             True, True)
+            if i == 3:
+                tOFF = ti(m)
+    need("s", "t", tA)
+    need("s", "v", vMQ)
+    sINJ = {}
+    for q in range(15, -1, -1):
+        sINJ[q] = si(s.activation(T.INJ[:, 256 * q:256 * q + 256], T.B2[:, 0:256], FN.Copy, scale=T.MASKQ[:, q:q + 1]))
+    vi(v.tensor_copy(T.DIAG[:], T.MASKQ[:]))
+    need("v", "ldidx", 32)
+    n1 = vi(v.tensor_scalar(T.PF[:, 10:11], T.PF[:, 4:5], 64.0, None, OP.mult))
+    need("v", "v", n1)
+    vID = vi(v.tensor_scalar(T.IDY[:], T.IDX[:], T.PF[:, 10:11], None, OP.add))
+    need("v", "t", tOFF)
+    last = [vi(v.tensor_copy(T.OFF[:, 128 * h:128 * h + 128], T.B1[:, 128 * h:128 * h + 128])) for h in range(2)]
+    src, base = T.INJ, 15 * 256
+    for n in range(15):
+        q = 14 - n
+        dst = (T.WA, T.WB)[n % 2]
+        need("v", "s", sINJ[q])
+        for h in range(2):
+            need("v", "v", last[h])
+            j = 16 * h + q
+            last[h] = vi(v.tensor_tensor(dst[:, 128 * h:128 * h + 128],
+                                         src[:, base + 128 * h:base + 128 * h + 128].indirect(T.OFF[:, 8 * j:8 * j + 8]),
+                                         T.INJ[:, 256 * q + 128 * h:256 * q + 128 * h + 128], OP.add))
+        src, base = dst, 0
+    H = src
+    vH0, vH = last
+    gi(g.iota(T.IO2G[:], [[2, 8]], 0, 0, allow_small_or_imprecise_dtypes=True))
+    gi(g.iota(T.IOR[:], [[2, 4]], 0, 0, allow_small_or_imprecise_dtypes=True))
+    n1 = gi(g.affine_select(T.R16A[:, 0::2], T.ONEF[:, 0::2], [[-16, 8]], OP.is_ge, 0.0, 0, 1))
+    gi(g.affine_select(T.R16[:, 1::2], T.ONEF[:, 1::2], [[-16, 8]], OP.is_equal, 0.0, -15, 1))
+    need("g", "gq", n1)
+    gR16 = gi(g.affine_select(T.R16[:, 0::2], T.R16A[:, 0::2], [[16, 8]], OP.is_ge, 0.0, 15, -1))
+    gi(g.affine_select(T.SELW[:], T.ONES[:, 0:192], [[1, 192]], OP.is_equal, 0.0, -32, -1))
+    n1 = gi(g.affine_select(T.BLKA[:], T.ONES[:, 0:128], [[-16, 8], [0, 16]], OP.is_ge, 0.0, 0, 1))
+    need("g", "gq", n1)
+    gBLK = gi(g.affine_select(T.BLK[:], T.BLKA[:], [[16, 8], [0, 16]], OP.is_ge, 0.0, 15, -1))
+    need("g", "ldem", 16)
+    need("g", "v", vID)
+    for h in range(2):
+        g.indirect_dma_start(T.AE[:, 128 * h:128 * h + 128], None, T.emd[:],
+                             IndirectOffsetOnAxis(ap=T.IDY[:, h:h + 1], axis=0), bounds_check=511).then_inc(S.ge, 16)
+    need("g", "gq", gBLK)
+    gi(g.affine_select(T.SHM[:], T.BLK[:], [[1, 128]], OP.is_equal, 0.0, -1, -1))
+    gi(g.affine_select(T.D0[:], T.SELW[:, 32:160], [[-16, 8], [0, 16]], OP.is_equal, 0.0, 0, 1))
+    gi(g.iota(T.IOTA2[:], [[0, 2], [1, 128]], 0, 0, allow_small_or_imprecise_dtypes=True))
+    gi(g.affine_select(T.TRI[:], T.BLK[:], [[1, 128]], OP.is_gt, 0.0, 0, -1))
+    n1 = gi(g.affine_select(T.B64A[:], T.ONES[:, 0:64], [[0, 8], [-16, 8]], OP.is_ge, 0.0, 0, 1))
+    gi(g.iota(T.MT[:], [[1, 4]], 0, 0, allow_small_or_imprecise_dtypes=True))
+    gi(g.iota(T.IOTAX[:, 0:131], [[1, 131]], -3, 0, allow_small_or_imprecise_dtypes=True))
+    need("g", "gq", n1)
+    gALL = gi(g.affine_select(T.B64[:], T.B64A[:], [[0, 8], [16, 8]], OP.is_ge, 0.0, 15, -1))
+    need("t", "gq", gR16)
+    need("t", "v", vH0)
+    vX = 0
+    if rank < N - 1:
+        t.matmul(T.B0[:, 0:16], H[:, 0:128], T.R16[:], True, True)
+        need("t", "v", vH)
+        tX = ti(t.matmul(T.B0[:, 16:32], H[:, 128:256], T.R16[:], True, True))
+        need("v", "t", tX)
+        n1 = vi(v.tensor_copy(T.XI[:], T.B0[:, 0:32:2]))
+        vi(v.tensor_scalar(T.XS[:, 0::2], T.B0[:, 1:32:2], 1.0 / 128, 128.0, OP.mult, OP.add))
+        need("v", "v", n1)
+        n1 = vi(v.tensor_scalar(T.XJ[:], T.XI[:], 127, None, OP.bitwise_and))
+        need("v", "v", n1)
+        vX = vi(v.tensor_scalar(T.XS[:, 1::2], T.XJ[:], -16.0, None, OP.add))
+        need("g", "v", vX)
+        nls = 0
+        for part in parts(topo, T, rank):
+            mask, ne = common_mask(topo, core, part, MOST)
+            g.remote_dma_fused([RemoteDMATransfer(dst_ids=[dst_id(topo, d) for d in part], dma_engine_mask=mask,
+                                                  remote_sem=S["arr%d" % rank], srcs=[T.XS[:]],
+                                                  dsts=[T.XR[:, 32 * rank:32 * rank + 32]] * len(part), alu_op=0)],
+                               local_sem=S.lsf)
+            nls += ne
+        g.wait_ge(S.lsf, nls)
+    need("v", "v", vH)
+    vTO = vi(v.tensor_scalar(T.TO[:], H[:], 1.0 / 128, 128.0, OP.mult, OP.add))
+    n1 = vi(v.tensor_copy(T.HI[:], H[:]))
+    need("v", "v", n1)
+    n1 = vi(v.tensor_scalar(T.HJ[:], T.HI[:], 127, None, OP.bitwise_and))
+    need("v", "v", n1)
+    vCO = vi(v.tensor_scalar(T.CO[:], T.HJ[:], -1.0, None, OP.add))
+    need("v", "gq", gALL)
+    n1 = vi(v.tensor_scalar(T.PF[:, 7:8], T.PF[:, 3:4], 8.0, T.PF[:, 2:3], OP.mult, OP.add))
+    vi(v.tensor_scalar(T.PF[:, 8:9], T.PF[:, 2:3], 129.0, -129.0, OP.mult, OP.add))
+    vSB = vi(v.tensor_scalar(T.PF[:, 9:10], T.MASKQ[:, 0:1], 129.0, -129.0, OP.mult, OP.add))
+    vi(v.tensor_scalar(T.REP[:], T.IOR[:], T.PF[:, 5:6], None, OP.add))
+    need("v", "v", n1)
+    vPM = vi(v.tensor_scalar(T.PERM[:], T.IO2G[:], T.PF[:, 7:8], None, OP.add))
+    need("t", "gq", gALL)
+    need("t", "v", vTO)
+    t.matmul(T.B3[:, 0:256], T.SHM[:], T.TO[:], True, False)
+    tS = ti(t.matmul(T.B3[:, 0:256], T.D0[:], T.IOTA2[:], False, True))
+    need("s", "t", tS)
+    need("s", "v", vSB)
+    sSO = si(s.activation(T.SO[:], T.B3[:, 0:256], FN.Identity, bias=T.PF[:, 9:10]))
+    ucol, L, vU, tail = T.U0[:, 0:1], 0, vPM, []
+    if rank > 0:
+        for r in range(min(rank, 4)):
+            arrived("v", r)
+        need("v", "v", vPM)
+        vQ = vi(v.tensor_copy(T.XQ1[:], T.XR[:, 0:128].indirect(T.PERM[:])))
+        need("t", "v", vQ)
+        tW = ti(t.matmul(T.B4[:, 0:128], T.XQ1[:], T.SELW[:, 32:160], True, True))
+        need("v", "t", tW)
+        vW = vi(v.tensor_scalar(T.WIN1[:], T.B4[:, 0:128], T.PF[:, 8:9], None, OP.add))
+        sW2 = 0
+        if nblk == 2:
+            arrived("s", 4)
+            need("s", "v", vPM)
+            sQ = si(s.activation(T.XQ2[:], T.XR[:, 128:256].indirect(T.PERM[:]), FN.Copy))
+            need("t", "s", sQ)
+            tW2 = ti(t.matmul(T.B5[:, 0:128], T.XQ2[:], T.SELW[:, 32:160], True, True))
+            need("s", "t", tW2)
+            sW2 = si(s.activation(T.WIN2[:], T.B5[:, 0:128], FN.Identity, bias=T.PF[:, 8:9]))
+        need("v", "v", vW)
+        need("s", "v", vW)
+        for k in range(2 * rank):
+            win = T.WIN1 if k < 8 else T.WIN2
+            qt = 2 * (k % 8)
+            if k == 8:
+                need("v", "s", sW2)
+                need("s", "s", sW2)
+            un = T.U[:, 16 * k:16 * k + 16]
+            need("v", "v", vU)
+            need("s", "v", vU)
+            vU = vi(v.tensor_copy(un, win[:, 0:128].indirect(ucol)))
+            sC = si(s.activation(T.CF[:, 16 * k:16 * k + 16], win[:, 0:128].indirect(ucol), FN.Copy,
+                                 scale=T.MASKQ[:, qt + 1:qt + 2]))
+            tail.append((T.CF[:, 16 * k + L:16 * k + L + 1], sC))
+            ucol, L = T.U[:, 16 * k + L:16 * k + L + 1], qt
+    need("v", "v", vU)
+    need("v", "s", sSO)
+    vM = vi(v.tensor_scalar(T.TM[:], T.TO[:, 0:128].indirect(ucol), -129.0, None, OP.add))
+    vSA = vi(v.tensor_copy(T.SA[:], T.SO[:, 0:128].indirect(ucol)))
+    need("s", "v", max(vU, vCO))
+    sCA = si(s.activation(T.CA[:], T.CO[:, 0:128].indirect(ucol), FN.Copy))
+    need("s", "v", vM)
+    sCC = si(s.activation(T.CC[:], T.CO[:, 128:256].indirect(T.TM[:, L:L + 1]), FN.Copy))
+    for bank in (T.B6, T.B7):
+        t.matmul(bank[:, 0:1], T.BLK[:], T.BC[:], True, False)
+    for col, sC in tail:
+        need("t", "s", sC)
+        for bank in (T.B6, T.B7):
+            t.matmul(bank[:, 0:1], T.BLK[:], col, False, False)
+    need("t", "s", sCA)
+    tB0 = ti(t.matmul(T.B6[:, 0:1], T.TRI[:], T.CA[:, L:L + 1], False, True))
+    t.matmul(T.B7[:, 0:1], T.BLK[:], T.CA[:, L:L + 1], False, False)
+    need("t", "s", sCC)
+    tB1 = ti(t.matmul(T.B7[:, 0:1], T.TRI[:], T.CC[:, 15:16], False, True))
+    need("v", "v", vM)
+    vSBk = vi(v.tensor_copy(T.SB[:, 1:17], T.SO[:, 128:256].indirect(T.TM[:, L:L + 1])))
+    v.wait_ge(S.ge, 32)
+    need("v", "v", vSA)
+    vE0 = vi(v.tensor_tensor(T.EM[:, 0:16], T.AE[:, 0:128].indirect(T.SA[:, L:L + 1]), T.DIAG[:], OP.mult))
+    need("v", "v", vSBk)
+    vE1 = vi(v.tensor_tensor(T.EM[:, 16:32], T.AE[:, 128:256].indirect(T.SB[:, 16:17]), T.DIAG[:], OP.mult))
+    need("v", "v", vE0)
+    vi(v.tensor_reduce(T.E2[:, 0:1], T.EM[:, 0:16], AxisListType.X, OP.max))
+    need("v", "s", sCA)
+    vi(v.tensor_scalar(T.GT[:, 0:4], T.MT[:], T.CA[:, L:L + 1], None, OP.is_lt))
+    need("v", "v", vE1)
+    vR1 = vi(v.tensor_reduce(T.E2[:, 1:2], T.EM[:, 16:32], AxisListType.X, OP.max))
+    need("v", "s", sCC)
+    vG1 = vi(v.tensor_scalar(T.GT[:, 4:8], T.MT[:], T.CC[:, 15:16], None, OP.is_lt))
+    need("v", "t", tB0)
+    vi(v.tensor_scalar(T.OH0[:, 0:131], T.IOTAX[:, 0:131], T.B6[:, 0:1], None, OP.is_equal))
+    need("v", "v", vG1)
+    vi(v.tensor_tensor(T.GTB[:], T.GT[:].indirect(T.REP[:]), T.B64[:], OP.mult))
+    need("v", "t", tB1)
+    vOH = vi(v.tensor_scalar(T.OH1[:, 0:131], T.IOTAX[:, 0:131], T.B7[:, 0:1], None, OP.is_equal))
+    need("v", "v", vR1)
+    vD = vi(v.tensor_scalar(T.D[:, 0::4], T.E2[:], 63, None, OP.bitwise_and))
+    for m in range(1, 4):
+        vD = vi(v.tensor_scalar(T.D[:, m::4], T.E2[:], 6 * m, 63, OP.logical_shift_right, OP.bitwise_and))
+    need("v", "v", vD)
+    vVB = vi(v.tensor_tensor(T.VB[:], T.D[:].indirect(T.REP[:]), T.GTB[:], OP.mult))
+    z = T.B1[:, 0:8]
+    need("t", "v", vOH)
+    for w, tile in enumerate((T.GTB, T.VB)):
+        if w:
+            need("t", "v", vVB)
+        for k in range(8):
+            m = k % 4
+            ins = t.matmul(z, (T.OH0, T.OH1)[k // 4][:, 3 - m:131 - m], tile[:, 8 * k:8 * k + 8],
+                           w == 0 and k == 0, w == 1 and k == 7)
+    tZ = ti(ins)
+    need("v", "t", tZ)
+    vZ = vi(v.tensor_copy(T.ZB[:], z))
+    need("g", "v", vZ)
+    near = beside(T, rank)
+    mask, ne = common_mask(topo, core, [T.cores[r] for r in near], MOST)
+    g.remote_dma_fused([RemoteDMATransfer(dst_ids=[dst_id(topo, T.cores[r]) for r in near], dma_engine_mask=mask,
+                                          remote_sem=S.arrz, srcs=[T.ZB[:]],
+                                          dsts=[(T.ZN if r < rank else T.ZP)[:] for r in near], alu_op=0)],
+                       local_sem=S.lsz)
+    g.wait_ge(S.lsz, ne)
+    o = T.B2[0:8, 0:64]
+    need("t", "v", vZ)
+    t.matmul(o, T.ZB[:], T.SELW[:, 64:128], True, False)
+    t.wait_ge(S.arrz, sum(common_mask(topo, T.cores[r], [T.cores[x] for x in beside(T, r)], MOST)[1] for r in near))
+    for n, r in enumerate(near):
+        c = 128 if r < rank else 0
+        ins = t.matmul(o, (T.ZP if r < rank else T.ZN)[:], T.SELW[:, c:c + 64], False, n == len(near) - 1)
+    tY = ti(ins)
+    need("v", "t", tY)
+    vY = vi(v.tensor_scalar(T.YS[0:8, :], o, -1.0, None, OP.add))
+    need("y", "v", vY)
+    y.dma_start(T.y[:], T.YS[0:8, :]).then_inc(S.st, 16)
+    y.wait_ge(S.st, 16)

@@ -3,13 +3,14 @@ from concourse.bass import IndirectOffsetOnAxis, DstId, RemoteDMATransfer
 
 SCRATCH = {"emd": ("dram", [512, 128], "int32")}
 for _t, _l in (
-    ("int32", "TN:32,16 TS:32,16 SY:8,16 XI:16 XJ:16 HI:256 HJ:256 IDX:2 IDY:2 AE:256 EM:32 E2:2 D:8 P:1 PI:8 DIAG:16"),
-    ("bfloat16", "TB:32,16 CB:32,16 TBLK:32,32 SYM:8,32 OA:128 O:128 OM:256 XS:32 XR:256 XQ1:128 XQ2:128 CF:160 TO:256 "
-                 "CO:256 CA:16 CC:16 GTB:64 VB:64 OH0:132 OH1:132 ZB:8 ZP:8 ZN:8 ONES:256 L2A:128 L2:128 SELW:192 BLKA:128 "
-                 "BLK:128 IOTA2:256 SHM:128 D0:128 TRI:128 B64A:64 B64:64 IOTAX:132 BC:1"),
-    ("uint16", "OFF:256 U0:2 U:160 TM:16 SA:16 SB:18 PERM:8 REP:4"),
-    ("float32", "INJ:4096 WA:256 WB:256 WIN1:128 WIN2:128 SO:256 GT:8 YS:64 ONEF:16 PF:12 IO16:16 MASKQ:16 IO2G:8 IOR:4 "
-                "R16A:16 R16:16 MT:4"),
+    ("int32", "TN:32,16 TS:32,16 SY:8,16 HI:256 HJ:256 IDX:2 IDY:2 AE:256 EM:32 E2:2 D:8 P:1 PI:8 DIAG:16"),
+    ("float16", "N16:32,16 OM:256"),
+    ("bfloat16", "TB:16,16 TBLK:32,32 SYM:8,32 OA:128 O:128 XS:32 XR:5,8,4 XQ1:8,16 XQ2:8,16 CF:160 TO:256 "
+                 "CO:256 CA:16 CC:16 GTB:64 VB:64 OH0:132 OH1:132 ZB:8 ZP:8 ZN:8 ONES:256 L2:128 SELW:192 BLKA:128 "
+                 "BLK:128 IOTA2:256 SHM:128 D0:128 TRI:128 IOTAX:132 BC:1 SELA:8 SELC:64 CONST:32"),
+    ("uint16", "OFF:256 U0:2 U:160 TM:16 SA:16 SB:18 REP:4"),
+    ("float32", "INJ:4096 WA:256 WB:256 WIN1:128 WIN2:128 SO:256 YS:64 ONEF:16 PF:12 PX:1 IO16:16 MASKQ:16 IOR:4 "
+                "SELT:64 MT0:32 MT1:32 MT:32 NEG:1 ROUND:1"),
 ):
     for _b in _l.split():
         _n, _d = _b.split(":")
@@ -21,6 +22,7 @@ SEMAPHORES = ["ldsy", "ldn0", "ldn1", "ldn2", "ldn3", "ldem", "ldidx", "v", "t",
 OP = AluOpType
 FN = ActivationFunctionType
 MOST = 8
+AHEAD = {0: 14, 1: 13, 2: 12, 3: 11, 4: 9, 6: 6, 9: 3, 12: 0}
 
 
 def common_mask(topo, src, dsts, most):
@@ -87,73 +89,94 @@ def rank_program(g, core, T, topo):
         (y, s)[i % 2].dma_start(T.TN[:, 8 * i:8 * i + 8, :], T.nx[2 * i:2 * i + 2, :]).then_inc(S["ldn%d" % i], 16)
     for h in range(2):
         y.dma_start(T.IDX[:, h:h + 1], T.sy[:, 16 * h:16 * h + 16]).then_inc(S.ldidx, 16)
+    y.wait_ge(S.ldn2, 16)
     y.dma_start(T.emd[:], T.em[:]).then_inc(S.ldem, 16)
 
-    vi(v.memset(T.ONES[:], 1.0))
-    v_ones = vi(v.memset(T.ONEF[:], 1.0))
-    gi(g.iota(T.P[:], [[1, 1]], 0, 1))
+    v_ones = vi(v.memset(T.ONES[:], 1.0))
+    gP = gi(g.iota(T.P[:], [[1, 1]], 0, 1))
     gIO = gi(g.iota(T.IO16[:], [[1, 16]], 0, 0, allow_small_or_imprecise_dtypes=True))
     need("g", "v", v_ones)
-    n1 = gi(g.affine_select(T.L2A[0:2, :], T.ONES[0:2, 0:128], [[1, 128]], OP.is_ge, 0.0, 0, -64))
-    need("g", "gq", n1)
-    gL2 = gi(g.affine_select(T.L2[0:2, :], T.L2A[0:2, :], [[-1, 128]], OP.is_ge, 0.0, 63, 64))
+    gL2 = gi(g.affine_select(T.L2[0:2, :], T.ONES[0:2, 0:128], [[1, 2], [0, 64]], OP.is_equal, 0.0, 0, -1))
+    gPX = gi(g.iota(T.PX[:], [[1, 1]], 0, 1, allow_small_or_imprecise_dtypes=True))
     vi(v.memset(T.TBLK[:], 0.0))
-    vi(v.memset(T.U0[:], 0))
-    vi(v.memset(T.BC[:], 2.0 - 4.0 * rank))
-    nblk = 0 if rank == 0 else (2 if rank > 4 else 1)
-    if nblk and 32 * rank < 128 * nblk:
-        vi(v.memset(T.XR[:, 32 * rank:128 * nblk], 0.0))
-    need("v", "gq", gIO)
-    for k, a in enumerate((15, 63, 1, 14)):
-        vi(v.tensor_scalar(T.PI[:, k:k + 1], T.P[:], a, None, OP.bitwise_and))
-    vi(v.tensor_scalar(T.PI[:, 4:5], T.P[:], 4, None, OP.logical_shift_right))
-    vP = vi(v.tensor_scalar(T.PI[:, 5:6], T.P[:], 3, 1, OP.logical_shift_right, OP.bitwise_and))
+    need("v", "gq", gP)
+    vi(v.tensor_scalar(T.PI[:, 0:1], T.P[:], 15, None, OP.bitwise_and))
+    vi(v.tensor_scalar(T.PI[:, 1:2], T.P[:], 4, None, OP.logical_shift_right))
+    vi(v.tensor_scalar(T.PI[:, 2:3], T.P[:], 3, 1, OP.logical_shift_right, OP.bitwise_and))
+    vP = vi(v.tensor_scalar(T.PI[:, 3:4], T.P[:], 63, None, OP.bitwise_and))
     need("v", "v", vP)
-    vi(v.tensor_copy(T.PF[:, 0:6], T.PI[:, 0:6]))
-    vPF = vi(v.tensor_copy(T.PF[:, 6:7], T.P[:]))
+    vPF = vi(v.tensor_copy(T.PF[:, 0:4], T.PI[:, 0:4]))
+    need("v", "gq", gIO)
     need("v", "v", vPF)
     vMQ = vi(v.tensor_scalar(T.MASKQ[:], T.IO16[:], T.PF[:, 0:1], None, OP.is_equal))
     need("v", "ldsy", 32)
-    vi(v.tensor_copy(T.SYM[0:2, :, 0:16], T.SY[0:2, :, :]))
-    vSY = vi(v.tensor_scalar(T.SYM[0:2, :, 16:32], T.SY[0:2, :, :], 64.0, None, OP.add))
+    vS0 = vi(v.tensor_copy(T.SYM[0:2, :, 0:16], T.SY[0:2, :, :]))
+    vS1 = vi(v.tensor_scalar(T.SYM[0:2, :, 16:32], T.SY[0:2, :, :], 64.0, None, OP.add))
     need("t", "gq", gL2)
-    need("t", "v", vSY)
-    tSY = ti(t.matmul(T.B0[:, 0:256], T.L2[0:2, :], T.SYM[0:2, :, :], True, True))
+    need("t", "v", vS0)
     tSO = ti(t.matmul(T.B3[:, 0:128], T.L2[0:2, :], T.SYM[0:2, :, 0:16], True, True))
+    need("t", "v", vS1)
+    tSY = ti(t.matmul(T.B0[:, 0:256], T.L2[0:2, :], T.SYM[0:2, :, :], True, True))
     need("s", "t", tSO)
     need("s", "v", vPF)
-    s1 = si(s.activation(T.OA[:], T.B3[:, 0:128], FN.Abs, bias=T.PF[:, 1:2], scale=-1.0))
+    s1 = si(s.activation(T.OA[:], T.B3[:, 0:128], FN.Abs, bias=T.PF[:, 3:4], scale=-1.0))
     need("s", "s", s1)
-    si(s.activation(T.O[:], T.OA[:], FN.Relu, bias=1.0, scale=-1.0))
-    vTB, sBLK = {}, {}
-    for i in range(4):
+    sO = si(s.activation(T.O[:], T.OA[:], FN.Relu, bias=1.0, scale=-1.0))
+    vN, blk, vTS = {}, {}, {}
+
+    def rows16(i):
         r8 = slice(8 * i, 8 * i + 8)
         need("v", "ldn%d" % i, 16)
-        vTS = vi(v.tensor_scalar(T.TS[:, r8, :], T.TN[:, r8, :], 127, None, OP.bitwise_and))
-        if i == 0:
-            need("v", "t", tSY)
-            vi(v.tensor_scalar(T.OM[:], T.B0[:, 0:256], T.PF[:, 6:7], None, OP.is_equal))
-        vi(v.tensor_scalar(T.CB[:, r8, :], T.TN[:, r8, :], 1.0 / 128, 128.50390625, OP.mult, OP.add))
-        need("v", "v", vTS)
-        vTB[i] = vi(v.tensor_scalar(T.TB[:, r8, :], T.TS[:, r8, :], 128.0, None, OP.mult))
-        need("s", "v", vTB[i])
+        vN[i] = vi(v.tensor_copy(T.N16[:, r8, :], T.TN[:, r8, :]))
+
+    def states(i):
+        r8 = slice(8 * i, 8 * i + 8)
+        need("v", "ldn%d" % i, 16)
+        vTS[i] = vi(v.tensor_scalar(T.TS[:, r8, :], T.TN[:, r8, :], 127, None, OP.bitwise_and))
+
+    def blocks(i):
+        r8 = slice(8 * i, 8 * i + 8)
+        need("v", "v", vTS[i])
+        if i < 2:
+            n = vi(v.tensor_copy(T.TB[:, r8, :], T.TS[:, r8, :]))
+            need("s", "v", n)
         for x in range(2):
             p = slice(64 * x, 64 * x + 64)
-            sBLK[i] = si(s.activation(T.TBLK[p, r8, 16 * x:16 * x + 16], T.TB[p, r8, :], FN.Copy, scale=1.0 / 128))
+            o = T.TBLK[p, r8, 16 * x:16 * x + 16]
+            if i < 2:
+                blk[i] = ("s", si(s.activation(o, T.TB[p, r8, :], FN.Copy)))
+            else:
+                blk[i] = ("v", vi(v.tensor_copy(o, T.TS[p, r8, :])))
+
+    states(0)
+    rows16(0)
+    blocks(0)
+    need("v", "t", tSY)
+    need("v", "gq", gPX)
+    vOM = vi(v.tensor_scalar(T.OM[:], T.B0[:, 0:256], T.PX[:], None, OP.is_equal))
+    states(1)
+    rows16(1)
+    blocks(1)
+    rows16(2)
+    rows16(3)
+    states(2)
+    states(3)
+    blocks(2)
+    blocks(3)
     tA = tOFF = 0
-    for kind, i in (("A", 0), ("A", 1), ("F", 0), ("A", 2), ("F", 1), ("A", 3), ("F", 2), ("F", 3)):
+    for kind, i in (("A", 0), ("A", 1), ("A", 2), ("A", 3), ("F", 0), ("F", 1), ("F", 2), ("F", 3)):
         r8 = slice(8 * i, 8 * i + 8)
         if kind == "A":
-            need("t", "v", vTB[i])
+            need("t", "v", max(vOM, vN[i]))
             for h in range(2):
                 k = 2 * i + h
-                a = T.B2[32 * i:32 * i + 32, 128 * h:128 * h + 128]
-                t.matmul(a, T.OM[:, 32 * k:32 * k + 32], T.TB[:, r8, :], True, False)
-                m = t.matmul(a, T.OM[:, 32 * k:32 * k + 32], T.CB[:, r8, :], False, True)
+                m = t.matmul(T.B2[32 * i:32 * i + 32, 128 * h:128 * h + 128], T.OM[:, 32 * k:32 * k + 32], T.N16[:, r8, :],
+                             True, True)
             if i == 3:
                 tA = ti(m)
         else:
-            need("t", "s", sBLK[i])
+            need("t", "s", sO)
+            need("t", *blk[i])
             for c in range(8):
                 m = t.matmul(T.B1[32 * i:32 * i + 32, c:256:8], T.TBLK[:, 8 * i + c, :], T.O[:, 32 * i:32 * i + 32],
                              True, True)
@@ -164,18 +187,25 @@ def rank_program(g, core, T, topo):
     sINJ = {}
     for q in range(15, -1, -1):
         sINJ[q] = si(s.activation(T.INJ[:, 256 * q:256 * q + 256], T.B2[:, 0:256], FN.Copy, scale=T.MASKQ[:, q:q + 1]))
-    vi(v.tensor_copy(T.DIAG[:], T.MASKQ[:]))
+    v_onef = vi(v.memset(T.ONEF[:], 1.0))
+    vi(v.memset(T.SELT[:], 0.0))
+    vZT = vi(v.memset(T.SELC[:], 0.0))
     need("v", "ldidx", 32)
-    n1 = vi(v.tensor_scalar(T.PF[:, 10:11], T.PF[:, 4:5], 64.0, None, OP.mult))
+    n1 = vi(v.tensor_scalar(T.PF[:, 4:5], T.PF[:, 1:2], 64.0, None, OP.mult))
+    vi(v.memset(T.CONST[:, 0::2], 129.0))
+    vCN = vi(v.memset(T.CONST[:, 1::2], -16.125))
     need("v", "v", n1)
-    vID = vi(v.tensor_scalar(T.IDY[:], T.IDX[:], T.PF[:, 10:11], None, OP.add))
+    vID = vi(v.tensor_scalar(T.IDY[:], T.IDX[:], T.PF[:, 4:5], None, OP.add))
+    vi(v.memset(T.NEG[:], -129.0))
+    vRD = vi(v.memset(T.ROUND[:], 128.50390625))
     need("v", "t", tOFF)
     last = [vi(v.tensor_copy(T.OFF[:, 128 * h:128 * h + 128], T.B1[:, 128 * h:128 * h + 128])) for h in range(2)]
     src, base = T.INJ, 15 * 256
     for n in range(15):
         q = 14 - n
         dst = (T.WA, T.WB)[n % 2]
-        need("v", "s", sINJ[q])
+        if n in AHEAD:
+            need("v", "s", sINJ[AHEAD[n]])
         for h in range(2):
             need("v", "v", last[h])
             j = 16 * h + q
@@ -184,101 +214,123 @@ def rank_program(g, core, T, topo):
                                          T.INJ[:, 256 * q + 128 * h:256 * q + 128 * h + 128], OP.add))
         src, base = dst, 0
     H = src
-    vH0, vH = last
-    gi(g.iota(T.IO2G[:], [[2, 8]], 0, 0, allow_small_or_imprecise_dtypes=True))
+    vH = last
+    n1 = gi(g.affine_select(T.SELA[:], T.ONES[:, 0:8], [[-16, 8]], OP.is_ge, 0.0, 0, 1))
+    n2 = gi(g.affine_select(T.BLKA[:], T.ONES[:, 0:128], [[-16, 8], [0, 16]], OP.is_ge, 0.0, 0, 1))
+    n3 = gi(g.iota(T.MT0[:], [[1, 4], [0, 8]], 0, 0, allow_small_or_imprecise_dtypes=True))
+    n4 = gi(g.affine_select(T.SELW[:], T.ONES[:, 0:192], [[1, 192]], OP.is_equal, 0.0, -32, -1))
+    need("g", "gq", n2)
+    n2 = gi(g.affine_select(T.BLK[:], T.BLKA[:], [[16, 8], [0, 16]], OP.is_ge, 0.0, 15, -1))
+    need("g", "gq", n3)
+    n3 = gi(g.affine_select(T.MT1[:], T.MT0[:], [[0, 4], [-16, 8]], OP.is_ge, 100.0, 0, 1))
+    need("g", "gq", n4)
+    gi(g.affine_select(T.D0[:], T.SELW[:, 32:160], [[-16, 8], [0, 16]], OP.is_equal, 0.0, 0, 1))
+    need("g", "gq", n3)
+    gi(g.affine_select(T.MT[:], T.MT1[:], [[0, 4], [16, 8]], OP.is_ge, 100.0, 15, -1))
+    gi(g.affine_select(T.SHM[:], T.BLK[:], [[1, 128]], OP.is_equal, 0.0, -1, -1))
+    gi(g.iota(T.IOTA2[:], [[0, 2], [1, 128]], 0, 0, allow_small_or_imprecise_dtypes=True))
     gi(g.iota(T.IOR[:], [[2, 4]], 0, 0, allow_small_or_imprecise_dtypes=True))
-    n1 = gi(g.affine_select(T.R16A[:, 0::2], T.ONEF[:, 0::2], [[-16, 8]], OP.is_ge, 0.0, 0, 1))
-    gi(g.affine_select(T.R16[:, 1::2], T.ONEF[:, 1::2], [[-16, 8]], OP.is_equal, 0.0, -15, 1))
-    need("g", "gq", n1)
-    gR16 = gi(g.affine_select(T.R16[:, 0::2], T.R16A[:, 0::2], [[16, 8]], OP.is_ge, 0.0, 15, -1))
-    gi(g.affine_select(T.SELW[:], T.ONES[:, 0:192], [[1, 192]], OP.is_equal, 0.0, -32, -1))
-    n1 = gi(g.affine_select(T.BLKA[:], T.ONES[:, 0:128], [[-16, 8], [0, 16]], OP.is_ge, 0.0, 0, 1))
-    need("g", "gq", n1)
-    gBLK = gi(g.affine_select(T.BLK[:], T.BLKA[:], [[16, 8], [0, 16]], OP.is_ge, 0.0, 15, -1))
     need("g", "ldem", 16)
-    need("g", "v", vID)
+    need("g", "v", max(vID, vZT, v_onef))
     for h in range(2):
         g.indirect_dma_start(T.AE[:, 128 * h:128 * h + 128], None, T.emd[:],
                              IndirectOffsetOnAxis(ap=T.IDY[:, h:h + 1], axis=0), bounds_check=511).then_inc(S.ge, 16)
-    need("g", "gq", gBLK)
-    gi(g.affine_select(T.SHM[:], T.BLK[:], [[1, 128]], OP.is_equal, 0.0, -1, -1))
-    gi(g.affine_select(T.D0[:], T.SELW[:, 32:160], [[-16, 8], [0, 16]], OP.is_equal, 0.0, 0, 1))
-    gi(g.iota(T.IOTA2[:], [[0, 2], [1, 128]], 0, 0, allow_small_or_imprecise_dtypes=True))
-    gi(g.affine_select(T.TRI[:], T.BLK[:], [[1, 128]], OP.is_gt, 0.0, 0, -1))
-    n1 = gi(g.affine_select(T.B64A[:], T.ONES[:, 0:64], [[0, 8], [-16, 8]], OP.is_ge, 0.0, 0, 1))
-    gi(g.iota(T.MT[:], [[1, 4]], 0, 0, allow_small_or_imprecise_dtypes=True))
-    gi(g.iota(T.IOTAX[:, 0:131], [[1, 131]], -3, 0, allow_small_or_imprecise_dtypes=True))
-    need("g", "gq", n1)
-    gALL = gi(g.affine_select(T.B64[:], T.B64A[:], [[0, 8], [16, 8]], OP.is_ge, 0.0, 15, -1))
-    need("t", "gq", gR16)
-    need("t", "v", vH0)
-    vX = 0
     if rank < N - 1:
-        t.matmul(T.B0[:, 0:16], H[:, 0:128], T.R16[:], True, True)
-        need("t", "v", vH)
-        tX = ti(t.matmul(T.B0[:, 16:32], H[:, 128:256], T.R16[:], True, True))
+        gi(g.affine_select(T.SELT[:, 0:32:4], T.ONEF[:, 0:8], [[-16, 8]], OP.is_equal, 0.0, -15, 1))
+        gS = gi(g.affine_select(T.SELC[:, 1:32:4], T.SELA[:], [[16, 8]], OP.is_ge, 0.0, 15, -1))
+    gi(g.affine_select(T.TRI[:], T.BLK[:], [[1, 128]], OP.is_gt, 0.0, 0, -1))
+    gALL = gi(g.iota(T.IOTAX[:, 0:131], [[1, 131]], -3, 0, allow_small_or_imprecise_dtypes=True))
+    sSE = 0
+    if rank < N - 1:
+        need("s", "gq", gS)
+        si(s.activation(T.SELT[:, 34:64:4], T.SELT[:, 0:32:4], FN.Copy))
+        si(s.activation(T.SELC[:, 35:64:4], T.SELC[:, 1:32:4], FN.Copy))
+        si(s.activation(T.SELC[:, 0:32:4], T.SELT[:, 0:32:4], FN.Copy, scale=-128.0))
+        sSE = si(s.activation(T.SELC[:, 34:64:4], T.SELT[:, 0:32:4], FN.Copy, scale=-128.0))
+    need("s", "v", max(vRD, vH[0]))
+    sCO = si(s.activation(T.CO[:, 0:128], H[:, 0:128], FN.Identity, bias=T.ROUND[:], scale=1.0 / 128))
+    need("v", "v", vH[1])
+    vCO = vi(v.tensor_scalar(T.CO[:, 128:256], H[:, 128:256], 1.0 / 128, 128.50390625, OP.mult, OP.add))
+    if rank < N - 1:
+        o = T.B0[:, 0:32]
+        need("t", "v", max(vCN, v_ones))
+        t.matmul(o, T.ONES[:, 0:128], T.CONST[:], True, False)
+        need("t", "s", sSE)
+        need("t", "v", vH[0])
+        t.matmul(o, H[:, 0:128], T.SELT[:, 0:32], False, False)
+        need("t", "s", sCO)
+        t.matmul(o, T.CO[:, 0:128], T.SELC[:, 0:32], False, False)
+        need("t", "v", vH[1])
+        t.matmul(o, H[:, 128:256], T.SELT[:, 32:64], False, False)
+        need("t", "v", vCO)
+        tX = ti(t.matmul(o, T.CO[:, 128:256], T.SELC[:, 32:64], False, True))
         need("v", "t", tX)
-        n1 = vi(v.tensor_copy(T.XI[:], T.B0[:, 0:32:2]))
-        vi(v.tensor_scalar(T.XS[:, 0::2], T.B0[:, 1:32:2], 1.0 / 128, 128.0, OP.mult, OP.add))
-        need("v", "v", n1)
-        n1 = vi(v.tensor_scalar(T.XJ[:], T.XI[:], 127, None, OP.bitwise_and))
-        need("v", "v", n1)
-        vX = vi(v.tensor_scalar(T.XS[:, 1::2], T.XJ[:], -16.0, None, OP.add))
+        vX = vi(v.tensor_copy(T.XS[:], T.B0[:, 0:32]))
         need("g", "v", vX)
         nls = 0
         for part in parts(topo, T, rank):
             mask, ne = common_mask(topo, core, part, MOST)
             g.remote_dma_fused([RemoteDMATransfer(dst_ids=[dst_id(topo, d) for d in part], dma_engine_mask=mask,
                                                   remote_sem=S["arr%d" % rank], srcs=[T.XS[:]],
-                                                  dsts=[T.XR[:, 32 * rank:32 * rank + 32]] * len(part), alu_op=0)],
+                                                  dsts=[T.XR[:, rank, :, :]] * len(part), alu_op=0)],
                                local_sem=S.lsf)
             nls += ne
         g.wait_ge(S.lsf, nls)
-    need("v", "v", vH)
-    vTO = vi(v.tensor_scalar(T.TO[:], H[:], 1.0 / 128, 128.0, OP.mult, OP.add))
+    need("v", "v", vH[1])
     n1 = vi(v.tensor_copy(T.HI[:], H[:]))
+    vi(v.memset(T.BC[:], 2.0 - 4.0 * rank))
+    vi(v.memset(T.U0[:], 0))
     need("v", "v", n1)
     n1 = vi(v.tensor_scalar(T.HJ[:], T.HI[:], 127, None, OP.bitwise_and))
+    vXZ = vi(v.tensor_copy(T.DIAG[:], T.MASKQ[:]))
+    if rank:
+        vXZ = vi(v.memset(T.XQ1[:], 0.0))
+    if rank > 4:
+        vXZ = vi(v.memset(T.XQ2[:], 0.0))
     need("v", "v", n1)
-    vCO = vi(v.tensor_scalar(T.CO[:], T.HJ[:], -1.0, None, OP.add))
+    vTO = vi(v.tensor_copy(T.TO[:], T.HJ[:]))
     need("v", "gq", gALL)
-    n1 = vi(v.tensor_scalar(T.PF[:, 7:8], T.PF[:, 3:4], 8.0, T.PF[:, 2:3], OP.mult, OP.add))
-    vi(v.tensor_scalar(T.PF[:, 8:9], T.PF[:, 2:3], 129.0, -129.0, OP.mult, OP.add))
-    vSB = vi(v.tensor_scalar(T.PF[:, 9:10], T.MASKQ[:, 0:1], 129.0, -129.0, OP.mult, OP.add))
-    vi(v.tensor_scalar(T.REP[:], T.IOR[:], T.PF[:, 5:6], None, OP.add))
-    need("v", "v", n1)
-    vPM = vi(v.tensor_scalar(T.PERM[:], T.IO2G[:], T.PF[:, 7:8], None, OP.add))
+    vRP = vi(v.tensor_scalar(T.REP[:], T.IOR[:], T.PF[:, 2:3], None, OP.add))
     need("t", "gq", gALL)
     need("t", "v", vTO)
     t.matmul(T.B3[:, 0:256], T.SHM[:], T.TO[:], True, False)
     tS = ti(t.matmul(T.B3[:, 0:256], T.D0[:], T.IOTA2[:], False, True))
     need("s", "t", tS)
-    need("s", "v", vSB)
-    sSO = si(s.activation(T.SO[:], T.B3[:, 0:256], FN.Identity, bias=T.PF[:, 9:10]))
-    ucol, L, vU, tail = T.U0[:, 0:1], 0, vPM, []
+    sSO = si(s.activation(T.SO[:], T.B3[:, 0:256], FN.Copy))
+    ucol, L, vU, tail = T.U0[:, 0:1], 0, vRP, []
     if rank > 0:
+        need("v", "v", vXZ)
+        need("s", "v", vXZ)
+        sQ1 = 0
         for r in range(min(rank, 4)):
-            arrived("v", r)
-        need("v", "v", vPM)
-        vQ = vi(v.tensor_copy(T.XQ1[:], T.XR[:, 0:128].indirect(T.PERM[:])))
+            if r == 1 and rank > 3:
+                arrived("s", r)
+                sQ1 = si(s.activation(T.XQ1[:, :, 4 * r:4 * r + 4], T.XR[:, r, :, :], FN.Copy))
+            else:
+                arrived("v", r)
+                vQ = vi(v.tensor_copy(T.XQ1[:, :, 4 * r:4 * r + 4], T.XR[:, r, :, :]))
         need("t", "v", vQ)
-        tW = ti(t.matmul(T.B4[:, 0:128], T.XQ1[:], T.SELW[:, 32:160], True, True))
+        need("t", "s", sQ1)
+        tW = ti(t.matmul(T.B4[:, 0:128], T.XQ1[:, :, :], T.SELW[:, 32:160], True, True))
         need("v", "t", tW)
-        vW = vi(v.tensor_scalar(T.WIN1[:], T.B4[:, 0:128], T.PF[:, 8:9], None, OP.add))
+        vi(v.tensor_copy(T.U[:, 0:1], T.B4[:, 0:1]))
+        vW = vi(v.tensor_copy(T.WIN1[:], T.B4[:, 0:128]))
         sW2 = 0
-        if nblk == 2:
+        if rank > 4:
             arrived("s", 4)
-            need("s", "v", vPM)
-            sQ = si(s.activation(T.XQ2[:], T.XR[:, 128:256].indirect(T.PERM[:]), FN.Copy))
+            sQ = si(s.activation(T.XQ2[:, :, 0:4], T.XR[:, 4, :, :], FN.Copy))
             need("t", "s", sQ)
-            tW2 = ti(t.matmul(T.B5[:, 0:128], T.XQ2[:], T.SELW[:, 32:160], True, True))
+            tW2 = ti(t.matmul(T.B5[:, 0:128], T.XQ2[:, :, :], T.SELW[:, 32:160], True, True))
             need("s", "t", tW2)
-            sW2 = si(s.activation(T.WIN2[:], T.B5[:, 0:128], FN.Identity, bias=T.PF[:, 8:9]))
+            sW2 = si(s.activation(T.WIN2[:], T.B5[:, 0:128], FN.Copy))
         need("v", "v", vW)
         need("s", "v", vW)
-        for k in range(2 * rank):
+        sC = si(s.activation(T.CF[:, 0:1], T.WIN1[:, 0:1], FN.Copy, scale=T.MASKQ[:, 1:2]))
+        tail.append((T.CF[:, 0:1], sC))
+        ucol = T.U[:, 0:1]
+        for k in range(1, 2 * rank):
             win = T.WIN1 if k < 8 else T.WIN2
-            qt = 2 * (k % 8)
+            row = 2 * (k % 8)
             if k == 8:
                 need("v", "s", sW2)
                 need("s", "s", sW2)
@@ -287,17 +339,19 @@ def rank_program(g, core, T, topo):
             need("s", "v", vU)
             vU = vi(v.tensor_copy(un, win[:, 0:128].indirect(ucol)))
             sC = si(s.activation(T.CF[:, 16 * k:16 * k + 16], win[:, 0:128].indirect(ucol), FN.Copy,
-                                 scale=T.MASKQ[:, qt + 1:qt + 2]))
+                                 scale=T.MASKQ[:, row + 1:row + 2]))
             tail.append((T.CF[:, 16 * k + L:16 * k + L + 1], sC))
-            ucol, L = T.U[:, 16 * k + L:16 * k + L + 1], qt
+            ucol, L = T.U[:, 16 * k + L:16 * k + L + 1], row
+    need("s", "v", max(vU, vCO))
+    need("s", "s", sCO)
+    sCA = si(s.activation(T.CA[:], T.CO[:, 0:128].indirect(ucol), FN.Identity, bias=T.NEG[:]))
     need("v", "v", vU)
     need("v", "s", sSO)
-    vM = vi(v.tensor_scalar(T.TM[:], T.TO[:, 0:128].indirect(ucol), -129.0, None, OP.add))
+    vM = vi(v.tensor_copy(T.TM[:], T.HJ[:, 0:128].indirect(ucol)))
     vSA = vi(v.tensor_copy(T.SA[:], T.SO[:, 0:128].indirect(ucol)))
-    need("s", "v", max(vU, vCO))
-    sCA = si(s.activation(T.CA[:], T.CO[:, 0:128].indirect(ucol), FN.Copy))
     need("s", "v", vM)
-    sCC = si(s.activation(T.CC[:], T.CO[:, 128:256].indirect(T.TM[:, L:L + 1]), FN.Copy))
+    sCC = si(s.activation(T.CC[:], T.CO[:, 128:256].indirect(T.TM[:, L:L + 1]), FN.Identity, bias=T.NEG[:]))
+    need("t", "v", vXZ)
     for bank in (T.B6, T.B7):
         t.matmul(bank[:, 0:1], T.BLK[:], T.BC[:], True, False)
     for col, sC in tail:
@@ -313,35 +367,31 @@ def rank_program(g, core, T, topo):
     vSBk = vi(v.tensor_copy(T.SB[:, 1:17], T.SO[:, 128:256].indirect(T.TM[:, L:L + 1])))
     v.wait_ge(S.ge, 32)
     need("v", "v", vSA)
-    vE0 = vi(v.tensor_tensor(T.EM[:, 0:16], T.AE[:, 0:128].indirect(T.SA[:, L:L + 1]), T.DIAG[:], OP.mult))
+    vi(v.tensor_tensor(T.EM[:, 0:16], T.AE[:, 0:128].indirect(T.SA[:, L:L + 1]), T.DIAG[:], OP.mult))
     need("v", "v", vSBk)
     vE1 = vi(v.tensor_tensor(T.EM[:, 16:32], T.AE[:, 128:256].indirect(T.SB[:, 16:17]), T.DIAG[:], OP.mult))
-    need("v", "v", vE0)
+    need("v", "v", vE1 - 1)
     vi(v.tensor_reduce(T.E2[:, 0:1], T.EM[:, 0:16], AxisListType.X, OP.max))
     need("v", "s", sCA)
-    vi(v.tensor_scalar(T.GT[:, 0:4], T.MT[:], T.CA[:, L:L + 1], None, OP.is_lt))
+    vi(v.tensor_scalar(T.GTB[:, 0:32], T.MT[:], T.CA[:, L:L + 1], None, OP.is_lt))
     need("v", "v", vE1)
     vR1 = vi(v.tensor_reduce(T.E2[:, 1:2], T.EM[:, 16:32], AxisListType.X, OP.max))
-    need("v", "s", sCC)
-    vG1 = vi(v.tensor_scalar(T.GT[:, 4:8], T.MT[:], T.CC[:, 15:16], None, OP.is_lt))
     need("v", "t", tB0)
-    vi(v.tensor_scalar(T.OH0[:, 0:131], T.IOTAX[:, 0:131], T.B6[:, 0:1], None, OP.is_equal))
-    need("v", "v", vG1)
-    vi(v.tensor_tensor(T.GTB[:], T.GT[:].indirect(T.REP[:]), T.B64[:], OP.mult))
-    need("v", "t", tB1)
-    vOH = vi(v.tensor_scalar(T.OH1[:, 0:131], T.IOTAX[:, 0:131], T.B7[:, 0:1], None, OP.is_equal))
+    vO0 = vi(v.tensor_scalar(T.OH0[:, 0:131], T.IOTAX[:, 0:131], T.B6[:, 0:1], None, OP.is_equal))
+    need("v", "s", sCC)
+    vG1 = vi(v.tensor_scalar(T.GTB[:, 32:64], T.MT[:], T.CC[:, 15:16], None, OP.is_lt))
     need("v", "v", vR1)
-    vD = vi(v.tensor_scalar(T.D[:, 0::4], T.E2[:], 63, None, OP.bitwise_and))
+    vi(v.tensor_scalar(T.D[:, 0::4], T.E2[:], 63, None, OP.bitwise_and))
+    need("v", "t", tB1)
+    vO1 = vi(v.tensor_scalar(T.OH1[:, 0:131], T.IOTAX[:, 0:131], T.B7[:, 0:1], None, OP.is_equal))
     for m in range(1, 4):
         vD = vi(v.tensor_scalar(T.D[:, m::4], T.E2[:], 6 * m, 63, OP.logical_shift_right, OP.bitwise_and))
     need("v", "v", vD)
     vVB = vi(v.tensor_tensor(T.VB[:], T.D[:].indirect(T.REP[:]), T.GTB[:], OP.mult))
     z = T.B1[:, 0:8]
-    need("t", "v", vOH)
     for w, tile in enumerate((T.GTB, T.VB)):
-        if w:
-            need("t", "v", vVB)
         for k in range(8):
+            need("t", "v", vVB if w else (vO1 if k > 3 else max(vO0, vG1)))
             m = k % 4
             ins = t.matmul(z, (T.OH0, T.OH1)[k // 4][:, 3 - m:131 - m], tile[:, 8 * k:8 * k + 8],
                            w == 0 and k == 0, w == 1 and k == 7)

@@ -3,14 +3,15 @@ from concourse.bass import IndirectOffsetOnAxis, DstId, RemoteDMATransfer
 
 SCRATCH = {"emd": ("dram", [512, 128], "int32")}
 for _t, _l in (
-    ("int32", "TN:32,16 TS:32,16 SY:8,16 HI:256 HJ:256 IDX:2 IDY:2 AE:256 EM:32 E2:2 D:8 P:1 PI:8 DIAG:16"),
-    ("float16", "N16:32,16 OM:256"),
-    ("bfloat16", "TB:16,16 TBLK:32,32 SYM:8,32 OA:128 O:128 XS:32 XR:5,8,4 XQ1:8,16 XQ2:8,16 CF:160 TO:256 "
-                 "CO:256 CA:16 CC:16 GTB:64 VB:64 OH0:132 OH1:132 ZB:8 ZP:8 ZN:8 ONES:256 L2:128 SELW:192 BLKA:128 "
-                 "BLK:128 IOTA2:256 SHM:128 D0:128 TRI:128 IOTAX:132 BC:1 SELA:8 SELC:64 CONST:32"),
-    ("uint16", "OFF:256 U0:2 U:160 TM:16 SA:16 SB:18 REP:4"),
-    ("float32", "INJ:4096 WA:256 WB:256 WIN1:128 WIN2:128 SO:256 YS:64 ONEF:16 PF:12 PX:1 IO16:16 MASKQ:16 IOR:4 "
-                "SELT:64 MT0:32 MT1:32 MT:32 NEG:1 ROUND:1"),
+    ("int32", "TN:32,16 TS:32,16 SY:8,16 IDX:2 IDY:2 AE:256 EM:32 E2:2 D:8 P:1 PI:8 DIAG:16"),
+    ("float16", "N16:32,16 OM:256 HF:256 SELH:64 SHMH:128"),
+    ("bfloat16", "TB:16,16 TBLK:32,32 SYM:8,32 OA:128 O:128 XS:32 XR:5,8,4 XQ1:8,16 XQ2:8,16 CF:160 XM:128 "
+                 "CO:256 CZ:256 CO2:256 COC:128 CA:16 CC:16 GTB:64 VB:64 OH0:132 OH1:132 ZB:8 ZP:8 ZN:8 ONES:256 L2:128 "
+                 "SELW:192 BLKA:128 BLK:128 IOTA2:256 SHM:128 NSHM:128 D0:128 TRI:128 IOTAX:132 BC:1 SELC1:64 SELC2:64 "
+                 "SELC:64 SELT:64 CONST:32"),
+    ("uint16", "OFF:256 U0:2 U:160 SA:16 SB:16 REP:4 REP2:8 L16:8"),
+    ("float32", "INJ:4096 WA:256 WB:256 WIN1:128 WIN2:128 SO:256 SOC:128 YS:64 PF:12 PX:1 IO16:16 MASKQ:16 IOR:4 "
+                "IOG:8 II:128 MASKI:128 MT0:32 MT1:32 MT:32 NEG:1 ROUND:1 BI:1"),
 ):
     for _b in _l.split():
         _n, _d = _b.split(":")
@@ -22,7 +23,6 @@ SEMAPHORES = ["ldsy", "ldn0", "ldn1", "ldn2", "ldn3", "ldem", "ldidx", "v", "t",
 OP = AluOpType
 FN = ActivationFunctionType
 MOST = 8
-AHEAD = {0: 14, 1: 13, 2: 12, 3: 11, 4: 9, 6: 6, 9: 3, 12: 0}
 
 
 def common_mask(topo, src, dsts, most):
@@ -31,7 +31,7 @@ def common_mask(topo, src, dsts, most):
 
 
 def parts(topo, T, r):
-    me, later = T.cores[r], T.cores[r + 1:]
+    me, later = T.cores[r], T.cores[r + 1:][::-1]
     two = ([d for d in later if topo.chip(d) != topo.chip(me)], [d for d in later if topo.chip(d) == topo.chip(me)])
     return [p for p in two if p]
 
@@ -98,6 +98,7 @@ def rank_program(g, core, T, topo):
     need("g", "v", v_ones)
     gL2 = gi(g.affine_select(T.L2[0:2, :], T.ONES[0:2, 0:128], [[1, 2], [0, 64]], OP.is_equal, 0.0, 0, -1))
     gPX = gi(g.iota(T.PX[:], [[1, 1]], 0, 1, allow_small_or_imprecise_dtypes=True))
+    gST = gi(g.affine_select(T.SELT[:], T.ONES[:, 0:64], [[-2000, 2], [-16, 8], [1000, 4]], OP.is_equal, 0.0, -15, 1))
     vi(v.memset(T.TBLK[:], 0.0))
     need("v", "gq", gP)
     vi(v.tensor_scalar(T.PI[:, 0:1], T.P[:], 15, None, OP.bitwise_and))
@@ -187,25 +188,22 @@ def rank_program(g, core, T, topo):
     sINJ = {}
     for q in range(15, -1, -1):
         sINJ[q] = si(s.activation(T.INJ[:, 256 * q:256 * q + 256], T.B2[:, 0:256], FN.Copy, scale=T.MASKQ[:, q:q + 1]))
-    v_onef = vi(v.memset(T.ONEF[:], 1.0))
-    vi(v.memset(T.SELT[:], 0.0))
-    vZT = vi(v.memset(T.SELC[:], 0.0))
-    need("v", "ldidx", 32)
     n1 = vi(v.tensor_scalar(T.PF[:, 4:5], T.PF[:, 1:2], 64.0, None, OP.mult))
-    vi(v.memset(T.CONST[:, 0::2], 129.0))
-    vCN = vi(v.memset(T.CONST[:, 1::2], -16.125))
+    vRD = vi(v.memset(T.ROUND[:], 128.50390625))
+    vNG = vi(v.memset(T.NEG[:], -129.0))
+    need("v", "ldidx", 32)
     need("v", "v", n1)
     vID = vi(v.tensor_scalar(T.IDY[:], T.IDX[:], T.PF[:, 4:5], None, OP.add))
-    vi(v.memset(T.NEG[:], -129.0))
-    vRD = vi(v.memset(T.ROUND[:], 128.50390625))
+    need("v", "gq", gST)
+    vi(v.tensor_copy(T.SELH[:], T.SELT[:]))
     need("v", "t", tOFF)
     last = [vi(v.tensor_copy(T.OFF[:, 128 * h:128 * h + 128], T.B1[:, 128 * h:128 * h + 128])) for h in range(2)]
     src, base = T.INJ, 15 * 256
     for n in range(15):
         q = 14 - n
-        dst = (T.WA, T.WB)[n % 2]
-        if n in AHEAD:
-            need("v", "s", sINJ[AHEAD[n]])
+        dst = T.HF if n == 14 else (T.WA, T.WB)[n % 2]
+        need("v", "s", sINJ[q])
+        before, W = list(last), src
         for h in range(2):
             need("v", "v", last[h])
             j = 16 * h + q
@@ -215,57 +213,60 @@ def rank_program(g, core, T, topo):
         src, base = dst, 0
     H = src
     vH = last
-    n1 = gi(g.affine_select(T.SELA[:], T.ONES[:, 0:8], [[-16, 8]], OP.is_ge, 0.0, 0, 1))
     n2 = gi(g.affine_select(T.BLKA[:], T.ONES[:, 0:128], [[-16, 8], [0, 16]], OP.is_ge, 0.0, 0, 1))
     n3 = gi(g.iota(T.MT0[:], [[1, 4], [0, 8]], 0, 0, allow_small_or_imprecise_dtypes=True))
     n4 = gi(g.affine_select(T.SELW[:], T.ONES[:, 0:192], [[1, 192]], OP.is_equal, 0.0, -32, -1))
+    n6 = gi(g.affine_select(T.SELC1[:], T.ONES[:, 0:64], [[-2000, 2], [-16, 8], [1000, 4]], OP.is_ge, 0.0, -1000, 1))
     need("g", "gq", n2)
     n2 = gi(g.affine_select(T.BLK[:], T.BLKA[:], [[16, 8], [0, 16]], OP.is_ge, 0.0, 15, -1))
     need("g", "gq", n3)
     n3 = gi(g.affine_select(T.MT1[:], T.MT0[:], [[0, 4], [-16, 8]], OP.is_ge, 100.0, 0, 1))
-    need("g", "gq", n4)
+    need("g", "gq", n6)
+    n6 = gi(g.affine_select(T.SELC2[:], T.SELC1[:], [[2000, 2], [16, 8], [-1000, 4]], OP.is_ge, 0.0, 1015, -1))
     gi(g.affine_select(T.D0[:], T.SELW[:, 32:160], [[-16, 8], [0, 16]], OP.is_equal, 0.0, 0, 1))
-    need("g", "gq", n3)
+    need("g", "gq", n6)
+    gi(g.affine_select(T.SELC[:], T.SELC2[:], [[-2000, 2], [-16, 8], [1000, 4]], OP.not_equal, -128.0, -15, 1))
     gi(g.affine_select(T.MT[:], T.MT1[:], [[0, 4], [16, 8]], OP.is_ge, 100.0, 15, -1))
     gi(g.affine_select(T.SHM[:], T.BLK[:], [[1, 128]], OP.is_equal, 0.0, -1, -1))
     gi(g.iota(T.IOTA2[:], [[0, 2], [1, 128]], 0, 0, allow_small_or_imprecise_dtypes=True))
     gi(g.iota(T.IOR[:], [[2, 4]], 0, 0, allow_small_or_imprecise_dtypes=True))
+    gi(g.iota(T.IOG[:], [[4, 8]], 0, 0, allow_small_or_imprecise_dtypes=True))
+    gi(g.iota(T.CONST[:], [[0, 16], [-18576, 2]], 16512, 0, allow_small_or_imprecise_dtypes=True))
+    gC = gi(g.iota(T.II[:], [[0, 8], [1, 16]], 0, 0, allow_small_or_imprecise_dtypes=True))
     need("g", "ldem", 16)
-    need("g", "v", max(vID, vZT, v_onef))
+    need("g", "v", vID)
     for h in range(2):
         g.indirect_dma_start(T.AE[:, 128 * h:128 * h + 128], None, T.emd[:],
                              IndirectOffsetOnAxis(ap=T.IDY[:, h:h + 1], axis=0), bounds_check=511).then_inc(S.ge, 16)
-    if rank < N - 1:
-        gi(g.affine_select(T.SELT[:, 0:32:4], T.ONEF[:, 0:8], [[-16, 8]], OP.is_equal, 0.0, -15, 1))
-        gS = gi(g.affine_select(T.SELC[:, 1:32:4], T.SELA[:], [[16, 8]], OP.is_ge, 0.0, 15, -1))
-    gi(g.affine_select(T.TRI[:], T.BLK[:], [[1, 128]], OP.is_gt, 0.0, 0, -1))
-    gALL = gi(g.iota(T.IOTAX[:, 0:131], [[1, 131]], -3, 0, allow_small_or_imprecise_dtypes=True))
-    sSE = 0
-    if rank < N - 1:
-        need("s", "gq", gS)
-        si(s.activation(T.SELT[:, 34:64:4], T.SELT[:, 0:32:4], FN.Copy))
-        si(s.activation(T.SELC[:, 35:64:4], T.SELC[:, 1:32:4], FN.Copy))
-        si(s.activation(T.SELC[:, 0:32:4], T.SELT[:, 0:32:4], FN.Copy, scale=-128.0))
-        sSE = si(s.activation(T.SELC[:, 34:64:4], T.SELT[:, 0:32:4], FN.Copy, scale=-128.0))
-    need("s", "v", max(vRD, vH[0]))
-    sCO = si(s.activation(T.CO[:, 0:128], H[:, 0:128], FN.Identity, bias=T.ROUND[:], scale=1.0 / 128))
+    need("s", "v", vRD)
+    need("s", "s", sINJ[0])
+    si(s.activation(T.CZ[:], T.INJ[:, 0:256], FN.Identity, bias=T.ROUND[:], scale=1.0 / 128))
+    for h in range(2):
+        need("s", "v", before[h])
+        sCO = si(s.activation(T.CO[:, 128 * h:128 * h + 128], W[:, 128 * h:128 * h + 128].indirect(T.OFF[:, 128 * h:128 * h + 8]),
+                              FN.Identity, bias=T.ROUND[:], scale=1.0 / 128))
+    need("v", "gq", gC)
+    vMI = vi(v.tensor_scalar(T.MASKI[:], T.II[:], T.PF[:, 0:1], None, OP.is_equal))
+    vRP2 = vi(v.tensor_copy(T.REP2[:], T.IOG[:]))
     need("v", "v", vH[1])
-    vCO = vi(v.tensor_scalar(T.CO[:, 128:256], H[:, 128:256], 1.0 / 128, 128.50390625, OP.mult, OP.add))
+    vC2 = vi(v.tensor_scalar(T.CO2[:], H[:], 1.0 / 128, 128.50390625, OP.mult, OP.add))
+    o = T.B0[:, 0:32]
+    need("t", "gq", gC)
+    t.matmul(o, T.ONES[0:2, 0:128], T.CONST[0:2, :], True, False)
+    need("t", "s", sCO - 2)
+    for h in range(2):
+        t.matmul(o, T.CZ[:, 128 * h:128 * h + 128], T.SELC[:, 32 * h:32 * h + 32], False, False)
+    need("t", "s", sCO - 1)
+    t.matmul(o, T.CO[:, 0:128], T.SELC[:, 0:32], False, False)
+    need("t", "v", vH[0])
+    t.matmul(o, H[:, 0:128], T.SELH[:, 0:32], False, False)
+    need("t", "s", sCO)
+    t.matmul(o, T.CO[:, 128:256], T.SELC[:, 32:64], False, False)
+    need("t", "v", vH[1])
+    tX = ti(t.matmul(o, H[:, 128:256], T.SELH[:, 32:64], False, True))
+    need("v", "t", tX)
+    vX = vi(v.tensor_copy(T.XS[:], T.B0[:, 0:32]))
     if rank < N - 1:
-        o = T.B0[:, 0:32]
-        need("t", "v", max(vCN, v_ones))
-        t.matmul(o, T.ONES[:, 0:128], T.CONST[:], True, False)
-        need("t", "s", sSE)
-        need("t", "v", vH[0])
-        t.matmul(o, H[:, 0:128], T.SELT[:, 0:32], False, False)
-        need("t", "s", sCO)
-        t.matmul(o, T.CO[:, 0:128], T.SELC[:, 0:32], False, False)
-        need("t", "v", vH[1])
-        t.matmul(o, H[:, 128:256], T.SELT[:, 32:64], False, False)
-        need("t", "v", vCO)
-        tX = ti(t.matmul(o, T.CO[:, 128:256], T.SELC[:, 32:64], False, True))
-        need("v", "t", tX)
-        vX = vi(v.tensor_copy(T.XS[:], T.B0[:, 0:32]))
         need("g", "v", vX)
         nls = 0
         for part in parts(topo, T, rank):
@@ -275,29 +276,44 @@ def rank_program(g, core, T, topo):
                                                   dsts=[T.XR[:, rank, :, :]] * len(part), alu_op=0)],
                                local_sem=S.lsf)
             nls += ne
+    gi(g.affine_select(T.TRI[:], T.BLK[:], [[1, 128]], OP.is_gt, 0.0, 0, -1))
+    gALL = gi(g.iota(T.IOTAX[:, 0:131], [[1, 131]], -3, 0, allow_small_or_imprecise_dtypes=True))
+    if rank < N - 1:
         g.wait_ge(S.lsf, nls)
-    need("v", "v", vH[1])
-    n1 = vi(v.tensor_copy(T.HI[:], H[:]))
+    need("v", "v", max(vX, vMI, vRP2))
+    vXM = vi(v.tensor_tensor(T.XM[:], T.XS[:].indirect(T.REP2[:]), T.MASKI[:], OP.mult))
+    vi(v.tensor_copy(T.SHMH[:], T.SHM[:]))
+    vi(v.tensor_scalar(T.NSHM[:], T.SHM[:], -128.0, None, OP.mult))
+    vBI = vi(v.tensor_scalar(T.BI[:], T.PF[:, 0:1], 1.0, 16512.0, OP.min, OP.mult))
+    t.matmul(T.B3[:, 0:256], T.D0[:], T.IOTA2[:], True, False)
+    need("t", "v", vXM)
+    tL = ti(t.matmul(T.B2[:, 0:8], T.XM[:], T.BLK[:, 0::16], True, True))
+    need("t", "v", max(vBI, vC2))
+    t.matmul(T.B3[:, 0:256], T.SHMH[:], H[:], False, False)
+    tS = ti(t.matmul(T.B3[:, 0:256], T.NSHM[:], T.CO2[:], False, True))
     vi(v.memset(T.BC[:], 2.0 - 4.0 * rank))
     vi(v.memset(T.U0[:], 0))
-    need("v", "v", n1)
-    n1 = vi(v.tensor_scalar(T.HJ[:], T.HI[:], 127, None, OP.bitwise_and))
     vXZ = vi(v.tensor_copy(T.DIAG[:], T.MASKQ[:]))
     if rank:
         vXZ = vi(v.memset(T.XQ1[:], 0.0))
     if rank > 4:
         vXZ = vi(v.memset(T.XQ2[:], 0.0))
-    need("v", "v", n1)
-    vTO = vi(v.tensor_copy(T.TO[:], T.HJ[:]))
-    need("v", "gq", gALL)
     vRP = vi(v.tensor_scalar(T.REP[:], T.IOR[:], T.PF[:, 2:3], None, OP.add))
-    need("t", "gq", gALL)
-    need("t", "v", vTO)
-    t.matmul(T.B3[:, 0:256], T.SHM[:], T.TO[:], True, False)
-    tS = ti(t.matmul(T.B3[:, 0:256], T.D0[:], T.IOTA2[:], False, True))
+    need("v", "t", tL)
+    vL = vi(v.tensor_copy(T.L16[:], T.B2[:, 0:8]))
     need("s", "t", tS)
-    sSO = si(s.activation(T.SO[:], T.B3[:, 0:256], FN.Copy))
+    need("s", "v", vBI)
+    sSO = si(s.activation(T.SO[:], T.B3[:, 0:256], FN.Identity, bias=T.BI[:]))
+    need("s", "v", vL)
+    sCC = si(s.activation(T.COC[:], T.CO2[:, 128:256].indirect(T.L16[:]), FN.Copy))
+
+    def half1():
+        need("v", "s", sSO)
+        need("v", "v", vL)
+        return vi(v.tensor_copy(T.SOC[:], T.SO[:, 128:256].indirect(T.L16[:])))
     ucol, L, vU, tail = T.U0[:, 0:1], 0, vRP, []
+    if rank == 0:
+        vSOC = half1()
     if rank > 0:
         need("v", "v", vXZ)
         need("s", "v", vXZ)
@@ -309,6 +325,7 @@ def rank_program(g, core, T, topo):
             else:
                 arrived("v", r)
                 vQ = vi(v.tensor_copy(T.XQ1[:, :, 4 * r:4 * r + 4], T.XR[:, r, :, :]))
+        vSOC = half1()
         need("t", "v", vQ)
         need("t", "s", sQ1)
         tW = ti(t.matmul(T.B4[:, 0:128], T.XQ1[:, :, :], T.SELW[:, 32:160], True, True))
@@ -342,16 +359,17 @@ def rank_program(g, core, T, topo):
                                  scale=T.MASKQ[:, row + 1:row + 2]))
             tail.append((T.CF[:, 16 * k + L:16 * k + L + 1], sC))
             ucol, L = T.U[:, 16 * k + L:16 * k + L + 1], row
-    need("s", "v", max(vU, vCO))
-    need("s", "s", sCO)
-    sCA = si(s.activation(T.CA[:], T.CO[:, 0:128].indirect(ucol), FN.Identity, bias=T.NEG[:]))
-    need("v", "v", vU)
+    own = slice(L, L + 1)
+    need("s", "v", max(vU, vNG))
+    need("s", "s", sCC)
+    sCA = si(s.activation(T.CA[:], T.CO2[:, 0:128].indirect(ucol), FN.Identity, bias=T.NEG[:]))
+    sCC = si(s.activation(T.CC[:], T.COC[:].indirect(ucol), FN.Identity, bias=T.NEG[:]))
+    need("v", "v", max(vU, vSOC))
     need("v", "s", sSO)
-    vM = vi(v.tensor_copy(T.TM[:], T.HJ[:, 0:128].indirect(ucol)))
     vSA = vi(v.tensor_copy(T.SA[:], T.SO[:, 0:128].indirect(ucol)))
-    need("s", "v", vM)
-    sCC = si(s.activation(T.CC[:], T.CO[:, 128:256].indirect(T.TM[:, L:L + 1]), FN.Identity, bias=T.NEG[:]))
+    vSB = vi(v.tensor_copy(T.SB[:], T.SOC[:].indirect(ucol)))
     need("t", "v", vXZ)
+    need("t", "gq", gALL)
     for bank in (T.B6, T.B7):
         t.matmul(bank[:, 0:1], T.BLK[:], T.BC[:], True, False)
     for col, sC in tail:
@@ -359,33 +377,32 @@ def rank_program(g, core, T, topo):
         for bank in (T.B6, T.B7):
             t.matmul(bank[:, 0:1], T.BLK[:], col, False, False)
     need("t", "s", sCA)
-    tB0 = ti(t.matmul(T.B6[:, 0:1], T.TRI[:], T.CA[:, L:L + 1], False, True))
-    t.matmul(T.B7[:, 0:1], T.BLK[:], T.CA[:, L:L + 1], False, False)
+    tB0 = ti(t.matmul(T.B6[:, 0:1], T.TRI[:], T.CA[:, own], False, True))
+    t.matmul(T.B7[:, 0:1], T.BLK[:], T.CA[:, own], False, False)
     need("t", "s", sCC)
-    tB1 = ti(t.matmul(T.B7[:, 0:1], T.TRI[:], T.CC[:, 15:16], False, True))
-    need("v", "v", vM)
-    vSBk = vi(v.tensor_copy(T.SB[:, 1:17], T.SO[:, 128:256].indirect(T.TM[:, L:L + 1])))
+    tB1 = ti(t.matmul(T.B7[:, 0:1], T.TRI[:], T.CC[:, own], False, True))
     v.wait_ge(S.ge, 32)
     need("v", "v", vSA)
-    vi(v.tensor_tensor(T.EM[:, 0:16], T.AE[:, 0:128].indirect(T.SA[:, L:L + 1]), T.DIAG[:], OP.mult))
-    need("v", "v", vSBk)
-    vE1 = vi(v.tensor_tensor(T.EM[:, 16:32], T.AE[:, 128:256].indirect(T.SB[:, 16:17]), T.DIAG[:], OP.mult))
+    vi(v.tensor_tensor(T.EM[:, 0:16], T.AE[:, 0:128].indirect(T.SA[:, own]), T.DIAG[:], OP.mult))
+    need("v", "v", vSB)
+    vE1 = vi(v.tensor_tensor(T.EM[:, 16:32], T.AE[:, 128:256].indirect(T.SB[:, own]), T.DIAG[:], OP.mult))
+    need("v", "s", sCA)
+    vi(v.tensor_scalar(T.GTB[:, 0:32], T.MT[:], T.CA[:, own], None, OP.is_lt))
     need("v", "v", vE1 - 1)
     vi(v.tensor_reduce(T.E2[:, 0:1], T.EM[:, 0:16], AxisListType.X, OP.max))
-    need("v", "s", sCA)
-    vi(v.tensor_scalar(T.GTB[:, 0:32], T.MT[:], T.CA[:, L:L + 1], None, OP.is_lt))
     need("v", "v", vE1)
     vR1 = vi(v.tensor_reduce(T.E2[:, 1:2], T.EM[:, 16:32], AxisListType.X, OP.max))
+    need("v", "s", sCC)
+    vG1 = vi(v.tensor_scalar(T.GTB[:, 32:64], T.MT[:], T.CC[:, own], None, OP.is_lt))
+    need("v", "gq", gALL)
     need("v", "t", tB0)
     vO0 = vi(v.tensor_scalar(T.OH0[:, 0:131], T.IOTAX[:, 0:131], T.B6[:, 0:1], None, OP.is_equal))
-    need("v", "s", sCC)
-    vG1 = vi(v.tensor_scalar(T.GTB[:, 32:64], T.MT[:], T.CC[:, 15:16], None, OP.is_lt))
     need("v", "v", vR1)
     vi(v.tensor_scalar(T.D[:, 0::4], T.E2[:], 63, None, OP.bitwise_and))
-    need("v", "t", tB1)
-    vO1 = vi(v.tensor_scalar(T.OH1[:, 0:131], T.IOTAX[:, 0:131], T.B7[:, 0:1], None, OP.is_equal))
     for m in range(1, 4):
         vD = vi(v.tensor_scalar(T.D[:, m::4], T.E2[:], 6 * m, 63, OP.logical_shift_right, OP.bitwise_and))
+    need("v", "t", tB1)
+    vO1 = vi(v.tensor_scalar(T.OH1[:, 0:131], T.IOTAX[:, 0:131], T.B7[:, 0:1], None, OP.is_equal))
     need("v", "v", vD)
     vVB = vi(v.tensor_tensor(T.VB[:], T.D[:].indirect(T.REP[:]), T.GTB[:], OP.mult))
     z = T.B1[:, 0:8]

from concourse.mybir import dt, AluOpType, AxisListType, ActivationFunctionType
from concourse.bass import IndirectOffsetOnAxis, DstId, RemoteDMATransfer

SCRATCH = {"emd": ("dram", [512, 128], "int32")}
for _t, _l in (
    ("int32", "TN:32,16 TS:32,16 SY:8,16 IDX:2 IDY:2 AE:256 EM:32 E2:2 D:8 P:1 PI:8 DIAG:16"),
    ("float16", "N16:32,16 OM:256 HF:256 SELH:64 SHMH:128"),
    ("bfloat16", "TB:16,16 TBLK:32,32 SYM:8,32 OA:128 O:128 XS:32 XR:5,8,4 XQ1:8,16 XQ2:8,16 CF:160 XM:128 "
                 "CO:256 CZ:256 CO2:256 COC:128 CA:16 CC:16 GTB:64 VB:64 OH0:132 OH1:132 ZB:8 ZP:8 ZN:8 ONES:256 L2:128 "
                 "SELW:192 BLKA:128 BLK:128 IOTA2:256 SHM:128 NSHM:128 D0:128 TRI:128 IOTAX:132 BC:1 SELC1:64 SELC2:64 "
                 "SELC:64 SELT:64 CONST:32"),
    ("uint16", "OFF:256 U0:2 U:160 SA:16 SB:16 REP:4 REP2:8 L16:8"),
    ("float32", "INJ:4096 WA:256 WB:256 WIN1:128 WIN2:128 SO:256 SOC:128 YS:64 PF:12 PX:1 IO16:16 MASKQ:16 IOR:4 "
                "IOG:8 II:128 MASKI:128 MT0:32 MT1:32 MT:32 NEG:1 ROUND:1 BI:1"),
):
    for _b in _l.split():
        _n, _d = _b.split(":")
        SCRATCH[_n] = ("sbuf", [128] + [int(_x) for _x in _d.split(",")], _t)
for _b in range(8):
    SCRATCH["B%d" % _b] = ("psum", [128, 512], "float32")
SEMAPHORES = ["ldsy", "ldn0", "ldn1", "ldn2", "ldn3", "ldem", "ldidx", "v", "t", "s", "gq", "ge",
              "arr0", "arr1", "arr2", "arr3", "arr4", "arrz", "lsf", "lsz", "st"]
OP = AluOpType
FN = ActivationFunctionType
MOST = 8


def common_mask(topo, src, dsts, most):
    ok = [e for e in topo.engines(src, dsts[0]) if all(e in topo.engines(src, d) for d in dsts)][:most]
    return sum(1 << e for e in ok), len(ok)


def parts(topo, T, r):
    me, later = T.cores[r], T.cores[r + 1:][::-1]
    two = ([d for d in later if topo.chip(d) != topo.chip(me)], [d for d in later if topo.chip(d) == topo.chip(me)])
    return [p for p in two if p]


def beside(T, r):
    return [x for x in (r - 1, r + 1) if 0 <= x < len(T.cores)]


def dst_id(topo, d):
    rid, pid, _ = topo.addr(d)
    return DstId(rid=rid, pnc=pid)


def rank_program(g, core, T, topo):
    rank = T.rank_of(core)
    if rank is None:
        return
    v, t, s, y = g.vector, g.tensor, g.scalar, g.sync
    S = T.sem
    N = len(T.cores)
    cnt = {"v": 0, "t": 0, "s": 0, "gq": 0}
    seen = {}
    queues = {"v": v, "t": t, "s": s, "y": y, "g": g}

    def inc(key, ins):
        ins.then_inc(S[key], 1)
        cnt[key] += 1
        return cnt[key]

    def vi(ins):
        return inc("v", ins)

    def ti(ins):
        return inc("t", ins)

    def si(ins):
        return inc("s", ins)

    def gi(ins):
        return inc("gq", ins)

    def need(q, key, n):
        if n and seen.get((q, key), 0) < n:
            queues[q].wait_ge(S[key], n)
            seen[(q, key)] = n

    def arrived(q, r):
        for p in parts(topo, T, r):
            if core in p:
                need(q, "arr%d" % r, common_mask(topo, T.cores[r], p, MOST)[1])

    y.dma_start(T.SY[0:1, :, :], T.sy[0::2, :]).then_inc(S.ldsy, 16)
    s.dma_start(T.SY[1:2, :, :], T.sy[1::2, :]).then_inc(S.ldsy, 16)
    for i in range(4):
        (y, s)[i % 2].dma_start(T.TN[:, 8 * i:8 * i + 8, :], T.nx[2 * i:2 * i + 2, :]).then_inc(S["ldn%d" % i], 16)
    for h in range(2):
        y.dma_start(T.IDX[:, h:h + 1], T.sy[:, 16 * h:16 * h + 16]).then_inc(S.ldidx, 16)
    y.wait_ge(S.ldn2, 16)
    y.dma_start(T.emd[:], T.em[:]).then_inc(S.ldem, 16)

    v_ones = vi(v.memset(T.ONES[:], 1.0))
    gP = gi(g.iota(T.P[:], [[1, 1]], 0, 1))
    gIO = gi(g.iota(T.IO16[:], [[1, 16]], 0, 0, allow_small_or_imprecise_dtypes=True))
    need("g", "v", v_ones)
    gL2 = gi(g.affine_select(T.L2[0:2, :], T.ONES[0:2, 0:128], [[1, 2], [0, 64]], OP.is_equal, 0.0, 0, -1))
    gPX = gi(g.iota(T.PX[:], [[1, 1]], 0, 1, allow_small_or_imprecise_dtypes=True))
    gST = gi(g.affine_select(T.SELT[:], T.ONES[:, 0:64], [[-2000, 2], [-16, 8], [1000, 4]], OP.is_equal, 0.0, -15, 1))
    vi(v.memset(T.TBLK[:], 0.0))
    need("v", "gq", gP)
    vi(v.tensor_scalar(T.PI[:, 0:1], T.P[:], 15, None, OP.bitwise_and))
    vi(v.tensor_scalar(T.PI[:, 1:2], T.P[:], 4, None, OP.logical_shift_right))
    vi(v.tensor_scalar(T.PI[:, 2:3], T.P[:], 3, 1, OP.logical_shift_right, OP.bitwise_and))
    vP = vi(v.tensor_scalar(T.PI[:, 3:4], T.P[:], 63, None, OP.bitwise_and))
    need("v", "v", vP)
    vPF = vi(v.tensor_copy(T.PF[:, 0:4], T.PI[:, 0:4]))
    need("v", "gq", gIO)
    need("v", "v", vPF)
    vMQ = vi(v.tensor_scalar(T.MASKQ[:], T.IO16[:], T.PF[:, 0:1], None, OP.is_equal))
    need("v", "ldsy", 32)
    vS0 = vi(v.tensor_copy(T.SYM[0:2, :, 0:16], T.SY[0:2, :, :]))
    vS1 = vi(v.tensor_scalar(T.SYM[0:2, :, 16:32], T.SY[0:2, :, :], 64.0, None, OP.add))
    need("t", "gq", gL2)
    need("t", "v", vS0)
    tSO = ti(t.matmul(T.B3[:, 0:128], T.L2[0:2, :], T.SYM[0:2, :, 0:16], True, True))
    need("t", "v", vS1)
    tSY = ti(t.matmul(T.B0[:, 0:256], T.L2[0:2, :], T.SYM[0:2, :, :], True, True))
    need("s", "t", tSO)
    need("s", "v", vPF)
    s1 = si(s.activation(T.OA[:], T.B3[:, 0:128], FN.Abs, bias=T.PF[:, 3:4], scale=-1.0))
    need("s", "s", s1)
    sO = si(s.activation(T.O[:], T.OA[:], FN.Relu, bias=1.0, scale=-1.0))
    vN, blk, vTS = {}, {}, {}

    def rows16(i):
        r8 = slice(8 * i, 8 * i + 8)
        need("v", "ldn%d" % i, 16)
        vN[i] = vi(v.tensor_copy(T.N16[:, r8, :], T.TN[:, r8, :]))

    def states(i):
        r8 = slice(8 * i, 8 * i + 8)
        need("v", "ldn%d" % i, 16)
        vTS[i] = vi(v.tensor_scalar(T.TS[:, r8, :], T.TN[:, r8, :], 127, None, OP.bitwise_and))

    def blocks(i):
        r8 = slice(8 * i, 8 * i + 8)
        need("v", "v", vTS[i])
        if i < 2:
            n = vi(v.tensor_copy(T.TB[:, r8, :], T.TS[:, r8, :]))
            need("s", "v", n)
        for x in range(2):
            p = slice(64 * x, 64 * x + 64)
            o = T.TBLK[p, r8, 16 * x:16 * x + 16]
            if i < 2:
                blk[i] = ("s", si(s.activation(o, T.TB[p, r8, :], FN.Copy)))
            else:
                blk[i] = ("v", vi(v.tensor_copy(o, T.TS[p, r8, :])))

    states(0)
    rows16(0)
    blocks(0)
    need("v", "t", tSY)
    need("v", "gq", gPX)
    vOM = vi(v.tensor_scalar(T.OM[:], T.B0[:, 0:256], T.PX[:], None, OP.is_equal))
    states(1)
    rows16(1)
    blocks(1)
    rows16(2)
    rows16(3)
    states(2)
    states(3)
    blocks(2)
    blocks(3)
    tA = tOFF = 0
    for kind, i in (("A", 0), ("A", 1), ("A", 2), ("A", 3), ("F", 0), ("F", 1), ("F", 2), ("F", 3)):
        r8 = slice(8 * i, 8 * i + 8)
        if kind == "A":
            need("t", "v", max(vOM, vN[i]))
            for h in range(2):
                k = 2 * i + h
                m = t.matmul(T.B2[32 * i:32 * i + 32, 128 * h:128 * h + 128], T.OM[:, 32 * k:32 * k + 32], T.N16[:, r8, :],
                             True, True)
            if i == 3:
                tA = ti(m)
        else:
            need("t", "s", sO)
            need("t", *blk[i])
            for c in range(8):
                m = t.matmul(T.B1[32 * i:32 * i + 32, c:256:8], T.TBLK[:, 8 * i + c, :], T.O[:, 32 * i:32 * i + 32],
                             True, True)
            if i == 3:
                tOFF = ti(m)
    need("s", "t", tA)
    need("s", "v", vMQ)
    sINJ = {}
    for q in range(15, -1, -1):
        sINJ[q] = si(s.activation(T.INJ[:, 256 * q:256 * q + 256], T.B2[:, 0:256], FN.Copy, scale=T.MASKQ[:, q:q + 1]))
    n1 = vi(v.tensor_scalar(T.PF[:, 4:5], T.PF[:, 1:2], 64.0, None, OP.mult))
    vRD = vi(v.memset(T.ROUND[:], 128.50390625))
    vNG = vi(v.memset(T.NEG[:], -129.0))
    need("v", "ldidx", 32)
    need("v", "v", n1)
    vID = vi(v.tensor_scalar(T.IDY[:], T.IDX[:], T.PF[:, 4:5], None, OP.add))
    need("v", "gq", gST)
    vi(v.tensor_copy(T.SELH[:], T.SELT[:]))
    need("v", "t", tOFF)
    last = [vi(v.tensor_copy(T.OFF[:, 128 * h:128 * h + 128], T.B1[:, 128 * h:128 * h + 128])) for h in range(2)]
    src, base = T.INJ, 15 * 256
    for n in range(15):
        q = 14 - n
        dst = T.HF if n == 14 else (T.WA, T.WB)[n % 2]
        need("v", "s", sINJ[q])
        before, W = list(last), src
        for h in range(2):
            need("v", "v", last[h])
            j = 16 * h + q
            last[h] = vi(v.tensor_tensor(dst[:, 128 * h:128 * h + 128],
                                         src[:, base + 128 * h:base + 128 * h + 128].indirect(T.OFF[:, 8 * j:8 * j + 8]),
                                         T.INJ[:, 256 * q + 128 * h:256 * q + 128 * h + 128], OP.add))
        src, base = dst, 0
    H = src
    vH = last
    n2 = gi(g.affine_select(T.BLKA[:], T.ONES[:, 0:128], [[-16, 8], [0, 16]], OP.is_ge, 0.0, 0, 1))
    n3 = gi(g.iota(T.MT0[:], [[1, 4], [0, 8]], 0, 0, allow_small_or_imprecise_dtypes=True))
    n4 = gi(g.affine_select(T.SELW[:], T.ONES[:, 0:192], [[1, 192]], OP.is_equal, 0.0, -32, -1))
    n6 = gi(g.affine_select(T.SELC1[:], T.ONES[:, 0:64], [[-2000, 2], [-16, 8], [1000, 4]], OP.is_ge, 0.0, -1000, 1))
    need("g", "gq", n2)
    n2 = gi(g.affine_select(T.BLK[:], T.BLKA[:], [[16, 8], [0, 16]], OP.is_ge, 0.0, 15, -1))
    need("g", "gq", n3)
    n3 = gi(g.affine_select(T.MT1[:], T.MT0[:], [[0, 4], [-16, 8]], OP.is_ge, 100.0, 0, 1))
    need("g", "gq", n6)
    n6 = gi(g.affine_select(T.SELC2[:], T.SELC1[:], [[2000, 2], [16, 8], [-1000, 4]], OP.is_ge, 0.0, 1015, -1))
    gi(g.affine_select(T.D0[:], T.SELW[:, 32:160], [[-16, 8], [0, 16]], OP.is_equal, 0.0, 0, 1))
    need("g", "gq", n6)
    gi(g.affine_select(T.SELC[:], T.SELC2[:], [[-2000, 2], [-16, 8], [1000, 4]], OP.not_equal, -128.0, -15, 1))
    gi(g.affine_select(T.MT[:], T.MT1[:], [[0, 4], [16, 8]], OP.is_ge, 100.0, 15, -1))
    gi(g.affine_select(T.SHM[:], T.BLK[:], [[1, 128]], OP.is_equal, 0.0, -1, -1))
    gi(g.iota(T.IOTA2[:], [[0, 2], [1, 128]], 0, 0, allow_small_or_imprecise_dtypes=True))
    gi(g.iota(T.IOR[:], [[2, 4]], 0, 0, allow_small_or_imprecise_dtypes=True))
    gi(g.iota(T.IOG[:], [[4, 8]], 0, 0, allow_small_or_imprecise_dtypes=True))
    gi(g.iota(T.CONST[:], [[0, 16], [-18576, 2]], 16512, 0, allow_small_or_imprecise_dtypes=True))
    gC = gi(g.iota(T.II[:], [[0, 8], [1, 16]], 0, 0, allow_small_or_imprecise_dtypes=True))
    need("g", "ldem", 16)
    need("g", "v", vID)
    for h in range(2):
        g.indirect_dma_start(T.AE[:, 128 * h:128 * h + 128], None, T.emd[:],
                             IndirectOffsetOnAxis(ap=T.IDY[:, h:h + 1], axis=0), bounds_check=511).then_inc(S.ge, 16)
    need("s", "v", vRD)
    need("s", "s", sINJ[0])
    si(s.activation(T.CZ[:], T.INJ[:, 0:256], FN.Identity, bias=T.ROUND[:], scale=1.0 / 128))
    for h in range(2):
        need("s", "v", before[h])
        sCO = si(s.activation(T.CO[:, 128 * h:128 * h + 128], W[:, 128 * h:128 * h + 128].indirect(T.OFF[:, 128 * h:128 * h + 8]),
                              FN.Identity, bias=T.ROUND[:], scale=1.0 / 128))
    need("v", "gq", gC)
    vMI = vi(v.tensor_scalar(T.MASKI[:], T.II[:], T.PF[:, 0:1], None, OP.is_equal))
    vRP2 = vi(v.tensor_copy(T.REP2[:], T.IOG[:]))
    need("v", "v", vH[1])
    vC2 = vi(v.tensor_scalar(T.CO2[:], H[:], 1.0 / 128, 128.50390625, OP.mult, OP.add))
    o = T.B0[:, 0:32]
    need("t", "gq", gC)
    t.matmul(o, T.ONES[0:2, 0:128], T.CONST[0:2, :], True, False)
    need("t", "s", sCO - 2)
    for h in range(2):
        t.matmul(o, T.CZ[:, 128 * h:128 * h + 128], T.SELC[:, 32 * h:32 * h + 32], False, False)
    need("t", "s", sCO - 1)
    t.matmul(o, T.CO[:, 0:128], T.SELC[:, 0:32], False, False)
    need("t", "v", vH[0])
    t.matmul(o, H[:, 0:128], T.SELH[:, 0:32], False, False)
    need("t", "s", sCO)
    t.matmul(o, T.CO[:, 128:256], T.SELC[:, 32:64], False, False)
    need("t", "v", vH[1])
    tX = ti(t.matmul(o, H[:, 128:256], T.SELH[:, 32:64], False, True))
    need("v", "t", tX)
    vX = vi(v.tensor_copy(T.XS[:], T.B0[:, 0:32]))
    if rank < N - 1:
        need("g", "v", vX)
        nls = 0
        for part in parts(topo, T, rank):
            mask, ne = common_mask(topo, core, part, MOST)
            g.remote_dma_fused([RemoteDMATransfer(dst_ids=[dst_id(topo, d) for d in part], dma_engine_mask=mask,
                                                  remote_sem=S["arr%d" % rank], srcs=[T.XS[:]],
                                                  dsts=[T.XR[:, rank, :, :]] * len(part), alu_op=0)],
                               local_sem=S.lsf)
            nls += ne
    gi(g.affine_select(T.TRI[:], T.BLK[:], [[1, 128]], OP.is_gt, 0.0, 0, -1))
    gALL = gi(g.iota(T.IOTAX[:, 0:131], [[1, 131]], -3, 0, allow_small_or_imprecise_dtypes=True))
    if rank < N - 1:
        g.wait_ge(S.lsf, nls)
    need("v", "v", max(vX, vMI, vRP2))
    vXM = vi(v.tensor_tensor(T.XM[:], T.XS[:].indirect(T.REP2[:]), T.MASKI[:], OP.mult))
    vi(v.tensor_copy(T.SHMH[:], T.SHM[:]))
    vi(v.tensor_scalar(T.NSHM[:], T.SHM[:], -128.0, None, OP.mult))
    vBI = vi(v.tensor_scalar(T.BI[:], T.PF[:, 0:1], 1.0, 16512.0, OP.min, OP.mult))
    t.matmul(T.B3[:, 0:256], T.D0[:], T.IOTA2[:], True, False)
    need("t", "v", vXM)
    tL = ti(t.matmul(T.B2[:, 0:8], T.XM[:], T.BLK[:, 0::16], True, True))
    need("t", "v", max(vBI, vC2))
    t.matmul(T.B3[:, 0:256], T.SHMH[:], H[:], False, False)
    tS = ti(t.matmul(T.B3[:, 0:256], T.NSHM[:], T.CO2[:], False, True))
    vi(v.memset(T.BC[:], 2.0 - 4.0 * rank))
    vi(v.memset(T.U0[:], 0))
    vXZ = vi(v.tensor_copy(T.DIAG[:], T.MASKQ[:]))
    if rank:
        vXZ = vi(v.memset(T.XQ1[:], 0.0))
    if rank > 4:
        vXZ = vi(v.memset(T.XQ2[:], 0.0))
    vRP = vi(v.tensor_scalar(T.REP[:], T.IOR[:], T.PF[:, 2:3], None, OP.add))
    need("v", "t", tL)
    vL = vi(v.tensor_copy(T.L16[:], T.B2[:, 0:8]))
    need("s", "t", tS)
    need("s", "v", vBI)
    sSO = si(s.activation(T.SO[:], T.B3[:, 0:256], FN.Identity, bias=T.BI[:]))
    need("s", "v", vL)
    sCC = si(s.activation(T.COC[:], T.CO2[:, 128:256].indirect(T.L16[:]), FN.Copy))

    def half1():
        need("v", "s", sSO)
        need("v", "v", vL)
        return vi(v.tensor_copy(T.SOC[:], T.SO[:, 128:256].indirect(T.L16[:])))
    ucol, L, vU, tail = T.U0[:, 0:1], 0, vRP, []
    if rank == 0:
        vSOC = half1()
    if rank > 0:
        need("v", "v", vXZ)
        need("s", "v", vXZ)
        sQ1 = 0
        for r in range(min(rank, 4)):
            if r == 1 and rank > 3:
                arrived("s", r)
                sQ1 = si(s.activation(T.XQ1[:, :, 4 * r:4 * r + 4], T.XR[:, r, :, :], FN.Copy))
            else:
                arrived("v", r)
                vQ = vi(v.tensor_copy(T.XQ1[:, :, 4 * r:4 * r + 4], T.XR[:, r, :, :]))
        vSOC = half1()
        need("t", "v", vQ)
        need("t", "s", sQ1)
        tW = ti(t.matmul(T.B4[:, 0:128], T.XQ1[:, :, :], T.SELW[:, 32:160], True, True))
        need("v", "t", tW)
        vi(v.tensor_copy(T.U[:, 0:1], T.B4[:, 0:1]))
        vW = vi(v.tensor_copy(T.WIN1[:], T.B4[:, 0:128]))
        sW2 = 0
        if rank > 4:
            arrived("s", 4)
            sQ = si(s.activation(T.XQ2[:, :, 0:4], T.XR[:, 4, :, :], FN.Copy))
            need("t", "s", sQ)
            tW2 = ti(t.matmul(T.B5[:, 0:128], T.XQ2[:, :, :], T.SELW[:, 32:160], True, True))
            need("s", "t", tW2)
            sW2 = si(s.activation(T.WIN2[:], T.B5[:, 0:128], FN.Copy))
        need("v", "v", vW)
        need("s", "v", vW)
        sC = si(s.activation(T.CF[:, 0:1], T.WIN1[:, 0:1], FN.Copy, scale=T.MASKQ[:, 1:2]))
        tail.append((T.CF[:, 0:1], sC))
        ucol = T.U[:, 0:1]
        for k in range(1, 2 * rank):
            win = T.WIN1 if k < 8 else T.WIN2
            row = 2 * (k % 8)
            if k == 8:
                need("v", "s", sW2)
                need("s", "s", sW2)
            un = T.U[:, 16 * k:16 * k + 16]
            need("v", "v", vU)
            need("s", "v", vU)
            vU = vi(v.tensor_copy(un, win[:, 0:128].indirect(ucol)))
            sC = si(s.activation(T.CF[:, 16 * k:16 * k + 16], win[:, 0:128].indirect(ucol), FN.Copy,
                                 scale=T.MASKQ[:, row + 1:row + 2]))
            tail.append((T.CF[:, 16 * k + L:16 * k + L + 1], sC))
            ucol, L = T.U[:, 16 * k + L:16 * k + L + 1], row
    own = slice(L, L + 1)
    need("s", "v", max(vU, vNG))
    need("s", "s", sCC)
    sCA = si(s.activation(T.CA[:], T.CO2[:, 0:128].indirect(ucol), FN.Identity, bias=T.NEG[:]))
    sCC = si(s.activation(T.CC[:], T.COC[:].indirect(ucol), FN.Identity, bias=T.NEG[:]))
    need("v", "v", max(vU, vSOC))
    need("v", "s", sSO)
    vSA = vi(v.tensor_copy(T.SA[:], T.SO[:, 0:128].indirect(ucol)))
    vSB = vi(v.tensor_copy(T.SB[:], T.SOC[:].indirect(ucol)))
    need("t", "v", vXZ)
    need("t", "gq", gALL)
    for bank in (T.B6, T.B7):
        t.matmul(bank[:, 0:1], T.BLK[:], T.BC[:], True, False)
    for col, sC in tail:
        need("t", "s", sC)
        for bank in (T.B6, T.B7):
            t.matmul(bank[:, 0:1], T.BLK[:], col, False, False)
    need("t", "s", sCA)
    tB0 = ti(t.matmul(T.B6[:, 0:1], T.TRI[:], T.CA[:, own], False, True))
    t.matmul(T.B7[:, 0:1], T.BLK[:], T.CA[:, own], False, False)
    need("t", "s", sCC)
    tB1 = ti(t.matmul(T.B7[:, 0:1], T.TRI[:], T.CC[:, own], False, True))
    v.wait_ge(S.ge, 32)
    need("v", "v", vSA)
    vi(v.tensor_tensor(T.EM[:, 0:16], T.AE[:, 0:128].indirect(T.SA[:, own]), T.DIAG[:], OP.mult))
    need("v", "v", vSB)
    vE1 = vi(v.tensor_tensor(T.EM[:, 16:32], T.AE[:, 128:256].indirect(T.SB[:, own]), T.DIAG[:], OP.mult))
    need("v", "s", sCA)
    vi(v.tensor_scalar(T.GTB[:, 0:32], T.MT[:], T.CA[:, own], None, OP.is_lt))
    need("v", "v", vE1 - 1)
    vi(v.tensor_reduce(T.E2[:, 0:1], T.EM[:, 0:16], AxisListType.X, OP.max))
    need("v", "v", vE1)
    vR1 = vi(v.tensor_reduce(T.E2[:, 1:2], T.EM[:, 16:32], AxisListType.X, OP.max))
    need("v", "s", sCC)
    vG1 = vi(v.tensor_scalar(T.GTB[:, 32:64], T.MT[:], T.CC[:, own], None, OP.is_lt))
    need("v", "gq", gALL)
    need("v", "t", tB0)
    vO0 = vi(v.tensor_scalar(T.OH0[:, 0:131], T.IOTAX[:, 0:131], T.B6[:, 0:1], None, OP.is_equal))
    need("v", "v", vR1)
    vi(v.tensor_scalar(T.D[:, 0::4], T.E2[:], 63, None, OP.bitwise_and))
    for m in range(1, 4):
        vD = vi(v.tensor_scalar(T.D[:, m::4], T.E2[:], 6 * m, 63, OP.logical_shift_right, OP.bitwise_and))
    need("v", "t", tB1)
    vO1 = vi(v.tensor_scalar(T.OH1[:, 0:131], T.IOTAX[:, 0:131], T.B7[:, 0:1], None, OP.is_equal))
    need("v", "v", vD)
    vVB = vi(v.tensor_tensor(T.VB[:], T.D[:].indirect(T.REP[:]), T.GTB[:], OP.mult))
    z = T.B1[:, 0:8]
    for w, tile in enumerate((T.GTB, T.VB)):
        for k in range(8):
            need("t", "v", vVB if w else (vO1 if k > 3 else max(vO0, vG1)))
            m = k % 4
            ins = t.matmul(z, (T.OH0, T.OH1)[k // 4][:, 3 - m:131 - m], tile[:, 8 * k:8 * k + 8],
                           w == 0 and k == 0, w == 1 and k == 7)
    tZ = ti(ins)
    need("v", "t", tZ)
    vZ = vi(v.tensor_copy(T.ZB[:], z))
    need("g", "v", vZ)
    near = beside(T, rank)
    mask, ne = common_mask(topo, core, [T.cores[r] for r in near], MOST)
    g.remote_dma_fused([RemoteDMATransfer(dst_ids=[dst_id(topo, T.cores[r]) for r in near], dma_engine_mask=mask,
                                          remote_sem=S.arrz, srcs=[T.ZB[:]],
                                          dsts=[(T.ZN if r < rank else T.ZP)[:] for r in near], alu_op=0)],
                       local_sem=S.lsz)
    g.wait_ge(S.lsz, ne)
    o = T.B2[0:8, 0:64]
    need("t", "v", vZ)
    t.matmul(o, T.ZB[:], T.SELW[:, 64:128], True, False)
    t.wait_ge(S.arrz, sum(common_mask(topo, T.cores[r], [T.cores[x] for x in beside(T, r)], MOST)[1] for r in near))
    for n, r in enumerate(near):
        c = 128 if r < rank else 0
        ins = t.matmul(o, (T.ZP if r < rank else T.ZN)[:], T.SELW[:, c:c + 64], False, n == len(near) - 1)
    tY = ti(ins)
    need("v", "t", tY)
    vY = vi(v.tensor_scalar(T.YS[0:8, :], o, -1.0, None, OP.add))
    need("y", "v", vY)
    y.dma_start(T.y[:], T.YS[0:8, :]).then_inc(S.st, 16)
    y.wait_ge(S.st, 16)
